import numpy as np
import ml_dtypes


def mxq(x, axis, fmt="e4m3"):
    dtype, down = {"e4m3": (ml_dtypes.float8_e4m3fn, 7), "e5m2": (ml_dtypes.float8_e5m2, 14)}[fmt]
    v = np.moveaxis(np.asarray(x, np.float32).astype(ml_dtypes.bfloat16).astype(np.float64), axis, -1)
    blocks = v.reshape(v.shape[:-1] + (-1, 32))
    amax = np.abs(blocks).max(-1, keepdims=True)
    byte = np.maximum(np.where(amax > 0, np.frexp(amax)[1] - 1 + 127, 0) - down, 1)
    scale = np.exp2(byte - 127.0)
    codes = (blocks / scale).astype(np.float32).astype(dtype).astype(np.float64)
    return np.moveaxis((codes * scale).reshape(v.shape), -1, axis)


WIDE = False


def mx_kscale(k):
    if not WIDE:
        return np.ones(k)
    levels = np.array([10, -10, 5, -5, 0])
    if k % 512:
        return np.exp2(np.random.permutation(np.resize(levels, k // 32))).repeat(32)
    a = np.empty((k // 512, 16))
    for p in range(k // 512):
        a[p, :8] = np.random.permutation(np.resize(levels, 8))
        for g in range(8):
            far = levels[np.abs(levels - a[p, g]) >= 10]
            a[p, g + 8] = far[np.random.randint(len(far))]
    return np.exp2(a.ravel()).repeat(32)


BF16 = ml_dtypes.bfloat16


def bf(x):
    return np.asarray(x, np.float32).astype(BF16)


def f64(x):
    return np.asarray(x).astype(np.float64)


E2M1 = np.array([0.0, 0.5, 1.0, 1.5, 2.0, 3.0, 4.0, 6.0, -0.0, -0.5, -1.0, -1.5, -2.0, -3.0, -4.0, -6.0])


def pack_weight(w, fmt):
    k, n = w.shape
    w = f64(bf(w)).reshape(k // 32, 32, n)
    amax = np.abs(w).max(1)
    if fmt == "e4m3":
        byte = np.frexp(amax)[1] - 1 + 127 - 7
    else:
        mant, ex = np.frexp(amax / 6.0)
        byte = np.where(mant > 0.5, ex, ex - 1) + 127
    byte = np.clip(np.where(amax > 0, byte, 1), 1, 254)
    scaled = (w * np.exp2(127.0 - byte)[:, None, :]).reshape(k, n).astype(np.float32)
    by_word = np.ascontiguousarray(scaled.reshape(k // 512, 128, 4, n).transpose(0, 1, 3, 2))
    if fmt == "e4m3":
        words = by_word.astype(ml_dtypes.float8_e4m3fn).view(np.uint8)
    else:
        c = by_word.astype(ml_dtypes.float4_e2m1fn).view(np.uint8) & 0xF
        words = c[..., 0::2] | (c[..., 1::2] << 4)
    return np.ascontiguousarray(words), np.ascontiguousarray(byte.astype(np.uint8).reshape(k // 512, 16, n))


def unpack_weight(words, scales, fmt):
    g, p, n, _ = words.shape
    if fmt == "e4m3":
        vals = np.ascontiguousarray(words).view(ml_dtypes.float8_e4m3fn).astype(np.float64)
    else:
        nib = np.empty((g, p, n, 4), np.uint8)
        nib[..., 0::2] = words & 0xF
        nib[..., 1::2] = words >> 4
        vals = E2M1[nib]
    vals = vals * np.repeat(np.exp2(scales.astype(np.float64) - 127.0), 8, axis=1)[..., None]
    return vals.transpose(0, 1, 3, 2).reshape(g * 512, n)
def pack4(w):
    words, scales = pack_weight(w, "e2m1")
    return words.reshape(words.shape[0], 128, -1), scales


def unpack4(words, scales):
    return unpack_weight(words.reshape(words.shape[0], 128, -1, 2), scales, "e2m1")


def planes(Y):
    n, m = Y.shape
    b = f64(bf(Y)).reshape(n // 32, 32, m)
    amax = np.abs(b).max(1)
    byte = np.clip(np.where(amax > 0, np.frexp(amax)[1] - 1 + 127 - 7, 1), 1, 254)
    codes = (b * np.exp2(127.0 - byte)[:, None, :]).reshape(n, m).astype(np.float32).astype(ml_dtypes.float8_e4m3fn).view(np.uint8)
    words = codes.reshape(n // 512, 128, 4, m).transpose(0, 1, 3, 2)
    return np.ascontiguousarray(words), np.ascontiguousarray(byte.astype(np.uint8).reshape(n // 512, 16, m))


U, V, J, I, T = 1024, 1024, 1024, 1536, 4
BETA = 50.0

def profiles(taste, items, spread):
    x = (taste[:, :, None] * items[None]).sum(1) / np.sqrt(T) + 0.5 * np.random.randn(taste.shape[0], J)
    x = spread[:, None] * (x - x.mean(1, keepdims=True))
    dev = np.sqrt((x ** 2).mean(1))
    return x / (dev[:, None] * np.sqrt(J)), dev

def setup_inputs():
    s, t = mx_kscale(J), mx_kscale(V)
    items = np.random.randn(T, J)
    xq, _ = profiles(np.random.randn(U, T), items, np.exp(0.3 * np.random.randn(U)))
    xn, dev = profiles(np.random.randn(V, T), items, np.exp(0.3 * np.random.randn(V)))
    n = np.random.poisson(J * np.random.uniform(0.2, 0.6, (V, 1)) * np.random.uniform(0.2, 0.6, (1, U)))
    x_words, x_scales = pack_weight(xq.T / s[:, None], "e4m3")
    e_words, e_scales = pack4(0.25 * np.random.randn(J, I) / s[:, None])
    return {"x_words": x_words, "x_scales": x_scales, "prof": bf(xn * s[None, :]),
            "e_words": e_words, "e_scales": e_scales,
            "h": bf((n / (n + BETA)) ** 2 * t[:, None]), "dev": bf(dev / t),
            "conf": bf(100.0 / V * np.exp(0.3 * np.random.randn(U))),
            "gain": bf(np.exp(0.8 * np.random.randn(I))), "off": bf(0.3 * np.random.randn(I))}

def reference(x_words, x_scales, prof, e_words, e_scales, h, dev, conf, gain, off):
    b = mxq(f64(prof), 1, "e4m3")
    cos = b @ unpack_weight(x_words, x_scales, "e4m3")
    w = cos * np.abs(cos) * f64(h)
    c = (b @ unpack4(e_words, e_scales)) * f64(dev)[:, None]
    p = mxq(w, 0, "e4m3").T @ mxq(c, 0, "e4m3")
    y = p * f64(conf)[:, None] * f64(gain)[None, :] + f64(off)[None, :]
    Y = y.T
    words, scales = planes(Y)
    return y, words, scales

@@ -1,0 +1,408 @@
+from contextlib import ExitStack
+
+import concourse.mybir as mybir
+from concourse.masks import make_identity
+
+U, V, J, I = 1024, 1024, 1024, 1536
+FLOPS = 2 * V * J * U + 2 * V * J * I + 2 * U * V * I
+
+F32 = mybir.dt.float32
+BF16 = mybir.dt.bfloat16
+I32 = mybir.dt.int32
+U32 = mybir.dt.uint32
+U8 = mybir.dt.uint8
+FP8X4 = mybir.dt.float8_e4m3fn_x4
+FP4X4 = mybir.dt.float4_e2m1fn_x4
+ACT = mybir.ActivationFunctionType
+ALU = mybir.AluOpType
+
+P = 128
+PACK = 4
+GROUP = P * PACK
+JG, VG, UG, IG = J // GROUP, V // GROUP, U // GROUP, I // GROUP
+BANKS = 8
+LAG_W = 6
+LAG_ROUND = 6
+LAG_YQ = 12
+
+
+def tile_user_neighbour_rating_prediction_k4_kernel(
+    tc, x_words, x_scales, prof, e_words, e_scales, h, dev, conf, gain, off, out_0, out_1, out_2
+):
+    nc = tc.nc
+    with ExitStack() as ctx:
+        keep = ctx.enter_context(tc.tile_pool(name="keep", bufs=1))
+        work = ctx.enter_context(tc.tile_pool(name="work", bufs=3))
+        psum = ctx.enter_context(tc.psum_pool(name="psum", bufs=1))
+        ctx.enter_context(tc.manual_schedule())
+
+        def kept(name, shape, dtype):
+            return keep.tile(shape, dtype, name=name, align_bytes=64)
+
+        ident = kept("ident", [P, P], F32)
+        e_plane = kept("e_plane", [P, JG, I], U8)
+        x_plane = kept("x_plane", [P, U], U8)
+        nc.vector.memset(e_plane[:].rearrange("p g n -> p (g n)").bitcast(I32), 0)
+        nc.vector.memset(x_plane[:].bitcast(I32), 0)
+        make_identity(nc, ident[:])
+
+        prof_sb, x_sb, e_sb, h_sb = {}, {}, {}, {}
+
+        def load_prof(vg):
+            rows = prof[vg * GROUP : (vg + 1) * GROUP, :].rearrange("(m t) k -> m t k", t=PACK)
+            for t in range(PACK):
+                prof_sb[vg, t] = kept("prof_%d_%d" % (vg, t), [P, J], BF16)
+                nc.sync.dma_start(out=prof_sb[vg, t][:], in_=rows[:, t, :])
+
+        def load_x(ug):
+            x_sb[ug] = kept("x_%d" % ug, [P, JG, GROUP], U32)
+            src = x_words.rearrange("g p n t -> p g (n t)")[:, :, ug * GROUP * PACK : (ug + 1) * GROUP * PACK]
+            nc.sync.dma_start(out=x_sb[ug][:].bitcast(I32), in_=src.bitcast(I32))
+
+        def load_e(ig):
+            e_sb[ig] = kept("e_%d" % ig, [P, JG, 2 * GROUP], U8)
+            src = e_words.rearrange("g p b -> p g b")[:, :, ig * 2 * GROUP : (ig + 1) * 2 * GROUP]
+            nc.sync.dma_start(out=e_sb[ig][:].bitcast(I32), in_=src.bitcast(I32))
+
+        def load_h(vg, ug):
+            h_sb[vg, ug] = kept("h_%d_%d" % (vg, ug), [P, PACK, GROUP], BF16)
+            rows = h[vg * GROUP : (vg + 1) * GROUP, ug * GROUP : (ug + 1) * GROUP]
+            nc.sync.dma_start(out=h_sb[vg, ug][:], in_=rows.rearrange("(p t) u -> p t u", t=PACK))
+
+        dev_sb = kept("dev_sb", [P, VG, PACK], BF16)
+        gain_raw = kept("gain_raw", [P, IG, PACK], BF16)
+        off_raw = kept("off_raw", [P, IG, PACK], BF16)
+        conf_row = kept("conf_row", [P, U], BF16)
+        nc.gpsimd.dma_start(out=dev_sb[:], in_=dev.rearrange("(g p t) -> p g t", p=P, t=PACK))
+        for q in range(4):
+            nc.gpsimd.dma_start(
+                out=x_plane[32 * q : 32 * q + 4 * JG, :].bitcast(I32),
+                in_=x_scales[:, 4 * q : 4 * q + 4, :].bitcast(I32),
+            )
+
+        load_prof(0)
+        for q in range(4):
+            nc.sync.dma_start(
+                out=e_plane[32 * q : 32 * q + 4, :, :].bitcast(I32),
+                in_=e_scales[:, 4 * q : 4 * q + 4, :].rearrange("g r n -> r g n").bitcast(I32),
+            )
+        load_e(0)
+        load_x(0)
+        load_h(0, 0)
+        load_e(1)
+        load_prof(1)
+        load_h(1, 0)
+        load_x(1)
+        load_h(0, 1)
+        load_e(2)
+        load_h(1, 1)
+        nc.sync.dma_start(out=gain_raw[:], in_=gain.rearrange("(g p t) -> p g t", p=P, t=PACK))
+        nc.sync.dma_start(out=off_raw[:], in_=off.rearrange("(g p t) -> p g t", p=P, t=PACK))
+        nc.sync.dma_start(out=conf_row[:], in_=conf.partition_broadcast(P))
+
+        warm = kept("warm", [P, 1], F32)
+        nc.scalar.activation(out=warm[:], in_=ident[:, 0:1], func=ACT.Abs)
+
+        gain_f = kept("gain_f", [P, IG, PACK], F32)
+        off_f = kept("off_f", [P, IG, PACK], F32)
+        b_codes, b_plane = {}, {}
+        w_codes, w_plane, c_codes, c_plane = {}, {}, {}, {}
+        w_bf, c_bf, y_t, y_out = {}, {}, {}, {}
+        y_planes = [kept("y_plane_a", [P, U], U8), kept("y_plane_b", [P, U], U8)]
+
+        later = {}
+        clock = [0]
+
+        def after(lag, fn):
+            later.setdefault(clock[0] + lag, []).append(fn)
+
+        quantizers = {}
+
+        def quantize_next(*keys):
+            for key in keys:
+                later.setdefault(clock[0] + 1, []).append(quantizers[key])
+
+        def next_bank():
+            return psum.tile([P, PACK, P], F32, name="bank", tag="bank%d" % (clock[0] % BANKS))
+
+        def quantize(codes, plane, src):
+            nc.vector.quantize_mx(out=codes.bitcast(FP8X4), scales=plane, in_=src)
+
+        def turn_prof(vg, t):
+            bank = next_bank()
+            words = prof_sb[vg, t][:].bitcast(F32)
+            for jg in range(JG):
+                for e in range(2):
+                    nc.tensor.transpose(bank[:, 2 * jg + e, :], words[:, 256 * jg + e : 256 * (jg + 1) : 2], ident[:])
+            b_bf = work.tile([P, JG * GROUP], BF16, name="b_bf", align_bytes=64, bufs=4)
+            b_codes[vg, t] = kept("b_codes_%d_%d" % (vg, t), [P, JG, P], U32)
+            b_plane[vg, t] = kept("b_plane_%d_%d" % (vg, t), [P, JG, P], U8)
+
+            def leave():
+                nc.scalar.copy(
+                    out=b_bf[:].bitcast(F32).rearrange("p (g m e) -> p g m e", g=JG, e=2),
+                    in_=bank[:].rearrange("p (g e) m -> p g m e", e=2),
+                )
+
+            def quant():
+                quantize(
+                    b_codes[vg, t][:].rearrange("p g m -> p (g m)"), b_plane[vg, t][:].rearrange("p g m -> p (g m)"), b_bf[:]
+                )
+
+            after(1, leave)
+            after(2, quant)
+
+        def first_stage(vg, moving, planes):
+            bank = next_bank()
+            for t in range(PACK):
+                for jg in range(JG):
+                    nc.tensor.matmul_mx(
+                        out=bank[:, t, :],
+                        lhsT=b_codes[vg, t][:, jg, :].bitcast(FP8X4),
+                        lhsT_scale=b_plane[vg, t][:, jg, :],
+                        rhs=moving[jg],
+                        rhs_scale=planes[jg],
+                        start=(jg == 0),
+                        stop=(jg == JG - 1),
+                    )
+            return bank
+
+        def w_chunk(vg, ug, c):
+            cols = slice(c * P, (c + 1) * P)
+            u0 = ug * GROUP + c * P
+            bank = first_stage(
+                vg,
+                [x_sb[ug][:, jg, cols].bitcast(FP8X4) for jg in range(JG)],
+                [x_plane[4 * jg : P, u0 : u0 + P] for jg in range(JG)],
+            )
+            cos_h = work.tile([P, PACK, P], F32, name="cos_h", bufs=5)
+            size = work.tile([P, PACK, P], F32, name="size", bufs=5)
+            if c == 0:
+                w_bf[vg, ug] = work.tile([P, GROUP, PACK], BF16, name="w_bf", align_bytes=64, bufs=2)
+            dst = w_bf[vg, ug]
+
+            def shrink():
+                nc.vector.tensor_tensor(out=cos_h[:], in0=bank[:], in1=h_sb[vg, ug][:, :, cols], op=ALU.mult)
+
+            def magnitude():
+                nc.scalar.activation(out=size[:], in_=bank[:], func=ACT.Abs)
+
+            def weigh():
+                nc.gpsimd.tensor_tensor(
+                    out=dst[:, cols, :].rearrange("p (c i) t -> p c t i", i=2),
+                    in0=cos_h[:].rearrange("p t (c i) -> p c t i", i=2),
+                    in1=size[:].rearrange("p t (c i) -> p c t i", i=2),
+                    op=ALU.mult,
+                )
+
+            def quant():
+                w_codes[vg, ug] = kept("w_codes_%d_%d" % (vg, ug), [P, GROUP], U32)
+                w_plane[vg, ug] = kept("w_plane_%d_%d" % (vg, ug), [P, GROUP], U8)
+                quantize(w_codes[vg, ug][:], w_plane[vg, ug][:], dst[:].rearrange("p u t -> p (u t)"))
+
+            after(1, shrink)
+            after(2, magnitude)
+            after(3, weigh)
+            if c == PACK - 1:
+                quantizers["w", vg, ug] = quant
+
+        def c_chunk(vg, ig, c):
+            i0 = ig * GROUP + c * P
+            bank = first_stage(
+                vg,
+                [e_sb[ig][:, jg, 2 * c * P : 2 * (c + 1) * P].bitcast(FP4X4) for jg in range(JG)],
+                [e_plane[:, jg, i0 : i0 + P] for jg in range(JG)],
+            )
+            if c == 0:
+                c_bf[vg, ig] = work.tile([P, PACK, P, PACK], BF16, name="c_bf", align_bytes=64, bufs=3)
+            dst = c_bf[vg, ig]
+
+            def scale():
+                nc.vector.tensor_tensor(
+                    out=dst[:, :, 32 * c : 32 * (c + 1), :],
+                    in0=bank[:].rearrange("p t (m s) -> p s m t", s=PACK),
+                    in1=dev_sb[:, vg, :].rearrange("p (a b t) -> p a b t", a=1, b=1).to_broadcast([P, PACK, 32, PACK]),
+                    op=ALU.mult,
+                )
+
+            def quant():
+                c_codes[vg, ig] = kept("c_codes_%d_%d" % (vg, ig), [P, GROUP], U32)
+                c_plane[vg, ig] = kept("c_plane_%d_%d" % (vg, ig), [P, GROUP], U8)
+                quantize(c_codes[vg, ig][:], c_plane[vg, ig][:], dst[:].rearrange("p s m t -> p (s m t)"))
+
+            after(1, scale)
+            if c == PACK - 1:
+                quantizers["c", vg, ig] = quant
+
+        def second_stage(ig, ug, s, on_scalar):
+            bank = next_bank()
+            flat = bank[:].rearrange("p a b -> p (a b)")
+            cols = slice(s * P, (s + 1) * P)
+            for vg in range(VG):
+                nc.tensor.matmul_mx(
+                    out=flat,
+                    lhsT=c_codes[vg, ig][:, cols].bitcast(FP8X4),
+                    lhsT_scale=c_plane[vg, ig][:, cols],
+                    rhs=w_codes[vg, ug][:].bitcast(FP8X4),
+                    rhs_scale=w_plane[vg, ug][:],
+                    start=(vg == 0),
+                    stop=(vg == VG - 1),
+                )
+            p_conf = work.tile([P, GROUP], F32, name="p_conf", bufs=4)
+            if s == 0:
+                y_t[ig, ug] = work.tile([P, PACK, GROUP], F32, name="y_t", bufs=3)
+            dst = y_t[ig, ug]
+
+            def by_user():
+                nc.vector.tensor_tensor(out=p_conf[:], in0=flat, in1=conf_row[:, ug * GROUP : (ug + 1) * GROUP], op=ALU.mult)
+
+            def by_item():
+                if on_scalar:
+                    nc.scalar.activation(
+                        out=dst[:, s, :],
+                        in_=p_conf[:],
+                        func=ACT.Identity,
+                        scale=gain_f[:, ig, s : s + 1],
+                        bias=off_f[:, ig, s : s + 1],
+                    )
+                    return
+                nc.gpsimd.tensor_scalar(
+                    out=dst[:, s, :],
+                    in0=p_conf[:],
+                    scalar1=gain_f[:, ig, s : s + 1],
+                    scalar2=off_f[:, ig, s : s + 1],
+                    op0=ALU.mult,
+                    op1=ALU.add,
+                )
+
+            y_bf = []
+
+            def round_y(ub):
+                def run():
+                    if ub == 0:
+                        y_bf.append(work.tile([P, GROUP, PACK], BF16, name="y_bf", align_bytes=64, bufs=3))
+                    users = slice(ub * P, (ub + 1) * P)
+                    nc.scalar.copy(
+                        out=y_bf[0][:, users, :].rearrange("p (c i) t -> p c t i", i=2),
+                        in_=dst[:, :, users].rearrange("p t (c i) -> p c t i", i=2),
+                    )
+
+                return run
+
+            def quant():
+                y_codes = work.tile([P, GROUP], U32, name="y_codes", align_bytes=64, bufs=2)
+                row = 4 * (ig % 2)
+                plane = y_planes[ig // 2]
+                quantize(y_codes[:], plane[row:P, ug * GROUP : (ug + 1) * GROUP], y_bf[0][:].rearrange("p u t -> p (u t)"))
+                words = out_1[ig].rearrange("p m t -> p (m t)")[:, ug * GROUP * PACK : (ug + 1) * GROUP * PACK]
+                nc.sync.dma_start(out=words.bitcast(I32), in_=y_codes[:].bitcast(I32))
+                if ug == UG - 1 and ig >= 1:
+                    first = 2 * (ig // 2)
+                    for q in range(4):
+                        nc.sync.dma_start(
+                            out=out_2[first : ig + 1, 4 * q : 4 * q + 4, :].bitcast(I32),
+                            in_=plane[32 * q : 32 * q + row + 4, :].bitcast(I32),
+                        )
+
+            after(1, by_user)
+            after(2, by_item)
+            if s == PACK - 1:
+                for ub in range(PACK):
+                    quantizers["r", ig, ug, ub] = round_y(ub)
+                quantizers["y", ig, ug] = quant
+
+        def turn_y(ig, ug, ub, on_vector):
+            bank = next_bank()
+            for s in range(PACK):
+                nc.tensor.transpose(bank[:, s, :], y_t[ig, ug][:, s, ub * P : (ub + 1) * P], ident[:])
+            if ub % 2 == 0:
+                y_out[ig, ug] = work.tile([P, 2, GROUP], F32, name="y_out", bufs=5)
+            dst = y_out[ig, ug]
+
+            def leave():
+                rows = dst[:, ub % 2, :].rearrange("p (m s) -> p m s", s=PACK)
+                src = bank[:].rearrange("p s m -> p m s")
+                if on_vector:
+                    nc.vector.tensor_copy(out=rows, in_=src)
+                else:
+                    nc.scalar.copy(out=rows, in_=src)
+                if ub % 2 == 1:
+                    u0 = ug * GROUP + (ub - 1) * P
+                    block = out_0[u0 : u0 + 2 * P, ig * GROUP : (ig + 1) * GROUP]
+                    nc.sync.dma_start(out=block.rearrange("(b p) i -> p b i", p=P), in_=dst[:])
+
+            after(1, leave)
+
+        def weave(a, b):
+            merged = []
+            for k in range(max(len(a), len(b))):
+                merged.extend(a[k : k + 1])
+                merged.extend(b[k : k + 1])
+            return merged
+
+        def t_jobs(vg):
+            return [(turn_prof, vg, t) for t in range(PACK)]
+
+        def w_jobs(vg, ug):
+            return [(w_chunk, vg, ug, c) for c in range(PACK)]
+
+        def c_jobs(vg, ig):
+            return [(c_chunk, vg, ig, c) for c in range(PACK)]
+
+        def m_jobs(ig, ug, n_scalar):
+            return [(second_stage, ig, ug, s, s >= PACK - n_scalar) for s in range(PACK)]
+
+        def widen():
+            nc.scalar.copy(out=gain_f[:], in_=gain_raw[:])
+            nc.scalar.copy(out=off_f[:], in_=off_raw[:])
+
+        def then(job, *keys):
+            def run():
+                job[0](*job[1:])
+                quantize_next(*keys)
+
+            return (run,)
+
+        def closing(jobs, *keys):
+            return jobs[:-1] + [then(jobs[-1], *keys)]
+
+        def rounding(jobs, ig, ug):
+            return [then(job, ("r", ig, ug, ub)) for ub, job in enumerate(jobs[:PACK])] + jobs[PACK:]
+
+        def opening(jobs, *keys):
+            return [then(jobs[0], *keys)] + jobs[1:]
+
+        def r_jobs(ig, ug, n_vector):
+            return [(turn_y, ig, ug, ub, ub < n_vector) for ub in range(PACK)]
+
+        def idle():
+            return None
+
+        wait = [(idle,)]
+        def triples(cs, ws):
+            merged = []
+            for k in range(len(ws)):
+                merged.extend(cs[2 * k : 2 * k + 1] + ws[k : k + 1] + cs[2 * k + 1 : 2 * k + 2])
+            return merged
+
+        jobs = t_jobs(0) + wait + wait
+        jobs = jobs + weave(c_jobs(0, 0), w_jobs(0, 0)) + closing(c_jobs(0, 1)[:2], ("c", 0, 0))
+        jobs = jobs + opening(t_jobs(1), ("w", 0, 0)) + c_jobs(0, 1)[2:]
+        jobs = jobs + opening(weave(w_jobs(1, 0), c_jobs(1, 0)), ("c", 0, 1))
+        jobs = jobs + closing(c_jobs(1, 1), ("c", 1, 0), ("w", 1, 0)) + [(widen,)]
+        jobs = jobs + opening(weave(w_jobs(0, 1), c_jobs(0, 2)), ("c", 1, 1))
+        jobs = jobs + closing(m_jobs(0, 0, 2), ("c", 0, 2), ("w", 0, 1))
+        half = weave(w_jobs(1, 1), c_jobs(1, 2))
+        jobs = jobs + half[:4] + r_jobs(0, 0, 0) + half[4:]
+        jobs = jobs + closing(rounding(m_jobs(1, 0, 1), 0, 0), ("c", 1, 2), ("w", 1, 1))
+        jobs = jobs + wait + wait + closing(m_jobs(2, 0, 0), ("y", 0, 0)) + rounding(r_jobs(1, 0, 1), 1, 0)
+        jobs = jobs + closing(m_jobs(0, 1, 0), ("y", 1, 0)) + rounding(r_jobs(2, 0, 1), 2, 0)
+        jobs = jobs + closing(m_jobs(1, 1, 0), ("y", 2, 0)) + rounding(r_jobs(0, 1, 2), 0, 1)
+        jobs = jobs + closing(m_jobs(2, 1, 0), ("y", 0, 1)) + rounding(r_jobs(1, 1, 2), 1, 1) + wait + closing(wait, ("y", 1, 1))
+        jobs = jobs + rounding(r_jobs(2, 1, 3), 2, 1) + wait + closing(wait, ("y", 2, 1)) + wait * 2
+
+        for job in jobs:
+            for fn in later.get(clock[0], []):
+                fn()
+            job[0](*job[1:])
+            clock[0] = clock[0] + 1

@@ -21,6 +21,17 @@ PACK = 4
 GROUP = P * PACK
 JG, VG, UG, IG = J // GROUP, V // GROUP, U // GROUP, I // GROUP
 BANKS = 8
+ORDER = """
+i T00 T01+b00 T02+b01 T03+b02 i+b03+h000 i C000 C001+h001 W000 C002 W001 C003 T10 T11 W002+f001 T12 T13 W003
+C010+h100 C011+h101 i+B1+f003 C012 C013 W100 C100+c00+w00 W101 C101+f101 W102 C102+h010 W103 C103+h011+g
+W010+f103 C110 W011 C111 W012+c01+c10+w10+f011 C112+h110 W013 C113+h111 W110+f013 N000 W111 N001
+W112+c11+w01+f111 N002 W113 N003 C020+f113 C021 C022 C023 C120 R000+r000 R001+r001 C121+c02+w11 R002+r002
+R003+r003 M100 M101 C122+y00 M102 M103 C123 M010 M011 M012+c12 M013 R100+r100 R101+r101 M110 M111 R102+r102
+Q103+r103 M112 M113+y10 R010+r010 R011+r011 M200 M201 R012+r012 Q013+r013 M202 M203+y01 R110+r110 R111+r111
+M210 M211 R112+r112 Q113+r113 M212 M213+y11 R200+r200 R201+r201 R202+r202 Q203+r203 Q210+r210+y20 Q211+r211
+Q212+r212 R213+r213 i i+y21
+"""
+LOADS = "p0 s e0 h00 x0 p1 h10 e1 x1 h01 h11 e2"
 LAG_W = 6
 LAG_ROUND = 6
 LAG_YQ = 12
@@ -42,6 +53,7 @@ def tile_user_neighbour_rating_prediction_k4_kernel(
         ident = kept("ident", [P, P], F32)
         e_plane = kept("e_plane", [P, JG, I], U8)
         x_plane = kept("x_plane", [P, U], U8)
+        zeros = None
         nc.vector.memset(e_plane[:].rearrange("p g n -> p (g n)").bitcast(I32), 0)
         nc.vector.memset(x_plane[:].bitcast(I32), 0)
         make_identity(nc, ident[:])
@@ -80,22 +92,15 @@ def tile_user_neighbour_rating_prediction_k4_kernel(
                 in_=x_scales[:, 4 * q : 4 * q + 4, :].bitcast(I32),
             )
 
-        load_prof(0)
-        for q in range(4):
-            nc.sync.dma_start(
-                out=e_plane[32 * q : 32 * q + 4, :, :].bitcast(I32),
-                in_=e_scales[:, 4 * q : 4 * q + 4, :].rearrange("g r n -> r g n").bitcast(I32),
-            )
-        load_e(0)
-        load_x(0)
-        load_h(0, 0)
-        load_e(1)
-        load_prof(1)
-        load_h(1, 0)
-        load_x(1)
-        load_h(0, 1)
-        load_e(2)
-        load_h(1, 1)
+        def load_s():
+            for q in range(4):
+                nc.sync.dma_start(
+                    out=e_plane[32 * q : 32 * q + 4, :, :].bitcast(I32),
+                    in_=e_scales[:, 4 * q : 4 * q + 4, :].rearrange("g r n -> r g n").bitcast(I32),
+                )
+
+        for tok in LOADS.split():
+            {"s": load_s, "e": load_e, "x": load_x, "h": load_h, "p": load_prof}[tok[0]](*[int(ch) for ch in tok[1:]])
         nc.sync.dma_start(out=gain_raw[:], in_=gain.rearrange("(g p t) -> p g t", p=P, t=PACK))
         nc.sync.dma_start(out=off_raw[:], in_=off.rearrange("(g p t) -> p g t", p=P, t=PACK))
         nc.sync.dma_start(out=conf_row[:], in_=conf.partition_broadcast(P))
@@ -105,7 +110,7 @@ def tile_user_neighbour_rating_prediction_k4_kernel(
 
         gain_f = kept("gain_f", [P, IG, PACK], F32)
         off_f = kept("off_f", [P, IG, PACK], F32)
-        b_codes, b_plane = {}, {}
+        b_bf, b_codes, b_plane = {}, {}, {}
         w_codes, w_plane, c_codes, c_plane = {}, {}, {}, {}
         w_bf, c_bf, y_t, y_out = {}, {}, {}, {}
         y_planes = [kept("y_plane_a", [P, U], U8), kept("y_plane_b", [P, U], U8)]
@@ -128,29 +133,56 @@ def tile_user_neighbour_rating_prediction_k4_kernel(
         def quantize(codes, plane, src):
             nc.vector.quantize_mx(out=codes.bitcast(FP8X4), scales=plane, in_=src)
 
+        pair = [None, None]
+        h_words = {}
+
+        def interleave_h(vg, ug, half):
+            def run():
+                if half == 0:
+                    h_words[vg, ug] = work.tile([P, GROUP, PACK], BF16, name="h_words", bufs=3)
+                users = slice(half * 2 * P, (half + 1) * 2 * P)
+                nc.scalar.copy(
+                    out=h_words[vg, ug][:, users, :].rearrange("p (c i) t -> p c t i", i=4),
+                    in_=h_sb[vg, ug][:, :, users].rearrange("p t (c i) -> p c t i", i=4),
+                )
+
+            return run
+
+        for vg in range(VG):
+            for ug in range(UG):
+                for half in range(2):
+                    quantizers["h", vg, ug, half] = interleave_h(vg, ug, half)
+
         def turn_prof(vg, t):
             bank = next_bank()
             words = prof_sb[vg, t][:].bitcast(F32)
             for jg in range(JG):
                 for e in range(2):
                     nc.tensor.transpose(bank[:, 2 * jg + e, :], words[:, 256 * jg + e : 256 * (jg + 1) : 2], ident[:])
-            b_bf = work.tile([P, JG * GROUP], BF16, name="b_bf", align_bytes=64, bufs=4)
-            b_codes[vg, t] = kept("b_codes_%d_%d" % (vg, t), [P, JG, P], U32)
-            b_plane[vg, t] = kept("b_plane_%d_%d" % (vg, t), [P, JG, P], U8)
+            if t == 0:
+                b_bf[vg] = kept("b_bf_%d" % vg, [P, PACK, JG * GROUP], BF16)
+                b_codes[vg] = kept("b_codes_%d" % vg, [P, PACK, JG, P], U32)
+                b_plane[vg] = kept("b_plane_%d" % vg, [P, PACK, JG, P], U8)
 
             def leave():
                 nc.scalar.copy(
-                    out=b_bf[:].bitcast(F32).rearrange("p (g m e) -> p g m e", g=JG, e=2),
+                    out=b_bf[vg][:, t, :].bitcast(F32).rearrange("p (g m e) -> p g m e", g=JG, e=2),
                     in_=bank[:].rearrange("p (g e) m -> p g m e", e=2),
                 )
 
-            def quant():
-                quantize(
-                    b_codes[vg, t][:].rearrange("p g m -> p (g m)"), b_plane[vg, t][:].rearrange("p g m -> p (g m)"), b_bf[:]
-                )
+            def quant(first):
+                def run():
+                    quantize(
+                        b_codes[vg][:, first : t + 1].rearrange("p t g m -> p (t g m)"),
+                        b_plane[vg][:, first : t + 1].rearrange("p t g m -> p (t g m)"),
+                        b_bf[vg][:, first : t + 1].rearrange("p t k -> p (t k)"),
+                    )
+
+                return run
 
             after(1, leave)
-            after(2, quant)
+            quantizers["b", vg, t] = quant(t)
+            quantizers["B", vg] = quant(0)
 
         def first_stage(vg, moving, planes):
             bank = next_bank()
@@ -158,8 +190,8 @@ def tile_user_neighbour_rating_prediction_k4_kernel(
                 for jg in range(JG):
                     nc.tensor.matmul_mx(
                         out=bank[:, t, :],
-                        lhsT=b_codes[vg, t][:, jg, :].bitcast(FP8X4),
-                        lhsT_scale=b_plane[vg, t][:, jg, :],
+                        lhsT=b_codes[vg][:, t, jg, :].bitcast(FP8X4),
+                        lhsT_scale=b_plane[vg][:, t, jg, :],
                         rhs=moving[jg],
                         rhs_scale=planes[jg],
                         start=(jg == 0),
@@ -175,34 +207,34 @@ def tile_user_neighbour_rating_prediction_k4_kernel(
                 [x_sb[ug][:, jg, cols].bitcast(FP8X4) for jg in range(JG)],
                 [x_plane[4 * jg : P, u0 : u0 + P] for jg in range(JG)],
             )
-            cos_h = work.tile([P, PACK, P], F32, name="cos_h", bufs=5)
-            size = work.tile([P, PACK, P], F32, name="size", bufs=5)
-            if c == 0:
-                w_bf[vg, ug] = work.tile([P, GROUP, PACK], BF16, name="w_bf", align_bytes=64, bufs=2)
-            dst = w_bf[vg, ug]
+            if c % 2 == 0:
+                pair[0] = work.tile([P, 2 * P, PACK], F32, name="cos_h", bufs=3)
+                pair[1] = work.tile([P, 2 * P, PACK], F32, name="size", bufs=3)
+            cos_h, size = pair
+            half = slice((c % 2) * P, (c % 2 + 1) * P)
+            by_column = bank[:].rearrange("p t u -> p u t")
 
             def shrink():
-                nc.vector.tensor_tensor(out=cos_h[:], in0=bank[:], in1=h_sb[vg, ug][:, :, cols], op=ALU.mult)
+                nc.vector.tensor_tensor(out=cos_h[:, half, :], in0=by_column, in1=h_words[vg, ug][:, cols, :], op=ALU.mult)
 
             def magnitude():
-                nc.scalar.activation(out=size[:], in_=bank[:], func=ACT.Abs)
+                nc.scalar.activation(out=size[:, half, :], in_=by_column, func=ACT.Abs)
 
             def weigh():
-                nc.gpsimd.tensor_tensor(
-                    out=dst[:, cols, :].rearrange("p (c i) t -> p c t i", i=2),
-                    in0=cos_h[:].rearrange("p t (c i) -> p c t i", i=2),
-                    in1=size[:].rearrange("p t (c i) -> p c t i", i=2),
-                    op=ALU.mult,
-                )
+                if c == 1:
+                    w_bf[vg, ug] = work.tile([P, GROUP, PACK], BF16, name="w_bf", align_bytes=64, bufs=1)
+                dst = w_bf[vg, ug]
+                nc.gpsimd.tensor_tensor(out=dst[:, (c - 1) * P : (c + 1) * P, :], in0=cos_h[:], in1=size[:], op=ALU.mult)
 
             def quant():
                 w_codes[vg, ug] = kept("w_codes_%d_%d" % (vg, ug), [P, GROUP], U32)
                 w_plane[vg, ug] = kept("w_plane_%d_%d" % (vg, ug), [P, GROUP], U8)
-                quantize(w_codes[vg, ug][:], w_plane[vg, ug][:], dst[:].rearrange("p u t -> p (u t)"))
+                quantize(w_codes[vg, ug][:], w_plane[vg, ug][:], w_bf[vg, ug][:].rearrange("p u t -> p (u t)"))
 
             after(1, shrink)
             after(2, magnitude)
-            after(3, weigh)
+            if c % 2 == 1:
+                quantizers["f", vg, ug, c] = weigh
             if c == PACK - 1:
                 quantizers["w", vg, ug] = quant
 
@@ -219,9 +251,9 @@ def tile_user_neighbour_rating_prediction_k4_kernel(
 
             def scale():
                 nc.vector.tensor_tensor(
-                    out=dst[:, :, 32 * c : 32 * (c + 1), :],
-                    in0=bank[:].rearrange("p t (m s) -> p s m t", s=PACK),
-                    in1=dev_sb[:, vg, :].rearrange("p (a b t) -> p a b t", a=1, b=1).to_broadcast([P, PACK, 32, PACK]),
+                    out=dst[:, :, 32 * c : 32 * (c + 1), :].rearrange("p s m t -> p m s t"),
+                    in0=bank[:].rearrange("p t (m s) -> p m s t", s=PACK),
+                    in1=dev_sb[:, vg, :].rearrange("p (a b t) -> p a b t", a=1, b=1).to_broadcast([P, 32, PACK, PACK]),
                     op=ALU.mult,
                 )
 
@@ -283,8 +315,8 @@ def tile_user_neighbour_rating_prediction_k4_kernel(
                         y_bf.append(work.tile([P, GROUP, PACK], BF16, name="y_bf", align_bytes=64, bufs=3))
                     users = slice(ub * P, (ub + 1) * P)
                     nc.scalar.copy(
-                        out=y_bf[0][:, users, :].rearrange("p (c i) t -> p c t i", i=2),
-                        in_=dst[:, :, users].rearrange("p t (c i) -> p c t i", i=2),
+                        out=y_bf[0][:, users, :].rearrange("p (c i) t -> p c t i", i=4),
+                        in_=dst[:, :, users].rearrange("p t (c i) -> p c t i", i=4),
                     )
 
                 return run
@@ -375,6 +407,11 @@ def tile_user_neighbour_rating_prediction_k4_kernel(
         def r_jobs(ig, ug, n_vector):
             return [(turn_y, ig, ug, ub, ub < n_vector) for ub in range(PACK)]
 
+        def warm_up(n):
+            bank = next_bank()
+            for k in range(n):
+                nc.tensor.matmul(bank[:].rearrange("p a b -> p (a b)"), lhsT=zeros[:, :P], rhs=zeros[:], start=True, stop=True)
+
         def idle():
             return None
 
@@ -385,21 +422,28 @@ def tile_user_neighbour_rating_prediction_k4_kernel(
                 merged.extend(cs[2 * k : 2 * k + 1] + ws[k : k + 1] + cs[2 * k + 1 : 2 * k + 2])
             return merged
 
-        jobs = t_jobs(0) + wait + wait
-        jobs = jobs + weave(c_jobs(0, 0), w_jobs(0, 0)) + closing(c_jobs(0, 1)[:2], ("c", 0, 0))
-        jobs = jobs + opening(t_jobs(1), ("w", 0, 0)) + c_jobs(0, 1)[2:]
-        jobs = jobs + opening(weave(w_jobs(1, 0), c_jobs(1, 0)), ("c", 0, 1))
-        jobs = jobs + closing(c_jobs(1, 1), ("c", 1, 0), ("w", 1, 0)) + [(widen,)]
-        jobs = jobs + opening(weave(w_jobs(0, 1), c_jobs(0, 2)), ("c", 1, 1))
-        jobs = jobs + closing(m_jobs(0, 0, 2), ("c", 0, 2), ("w", 0, 1))
-        half = weave(w_jobs(1, 1), c_jobs(1, 2))
-        jobs = jobs + half[:4] + r_jobs(0, 0, 0) + half[4:]
-        jobs = jobs + closing(rounding(m_jobs(1, 0, 1), 0, 0), ("c", 1, 2), ("w", 1, 1))
-        jobs = jobs + wait + wait + closing(m_jobs(2, 0, 0), ("y", 0, 0)) + rounding(r_jobs(1, 0, 1), 1, 0)
-        jobs = jobs + closing(m_jobs(0, 1, 0), ("y", 1, 0)) + rounding(r_jobs(2, 0, 1), 2, 0)
-        jobs = jobs + closing(m_jobs(1, 1, 0), ("y", 2, 0)) + rounding(r_jobs(0, 1, 2), 0, 1)
-        jobs = jobs + closing(m_jobs(2, 1, 0), ("y", 0, 1)) + rounding(r_jobs(1, 1, 2), 1, 1) + wait + closing(wait, ("y", 1, 1))
-        jobs = jobs + rounding(r_jobs(2, 1, 3), 2, 1) + wait + closing(wait, ("y", 2, 1)) + wait * 2
+        jobs = []
+        for tok in ORDER.split():
+            parts = tok.split("+")
+            kind, d = parts[0][0], [int(ch) for ch in parts[0][1:]]
+            if kind == "T":
+                job = (turn_prof, d[0], d[1])
+            elif kind == "W":
+                job = (w_chunk, d[0], d[1], d[2])
+            elif kind == "C":
+                job = (c_chunk, d[0], d[1], d[2])
+            elif kind == "M" or kind == "N":
+                job = (second_stage, d[0], d[1], d[2], kind == "N")
+            elif kind == "R" or kind == "Q":
+                job = (turn_y, d[0], d[1], d[2], kind == "Q")
+            elif kind == "D":
+                job = (warm_up, d[0])
+            else:
+                job = (idle,)
+            keys = [tuple([p[0]] + [int(ch) for ch in p[1:]]) for p in parts[1:]]
+            jobs.append(then(job, *keys))
+        quantizers["g",] = widen
+        jobs = jobs + wait * 6
 
         for job in jobs:
             for fn in later.get(clock[0], []):

@@ -17,24 +17,12 @@ ACT = mybir.ActivationFunctionType
 ALU = mybir.AluOpType
 
 P = 128
-PACK = 4
-GROUP = P * PACK
+SLOTS = 4
+GROUP = P * SLOTS
 JG, VG, UG, IG = J // GROUP, V // GROUP, U // GROUP, I // GROUP
+QUADRANTS, QUADRANT, SCALE_ROWS = 4, 32, 4
 BANKS = 8
-ORDER = """
-i T00 T01+b00 T02+b01 T03+b02 i+b03+h000 i C000 C001+h001 W000 C002 W001 C003 T10 T11 W002+f001 T12 T13 W003
-C010+h100 C011+h101 i+B1+f003 C012 C013 W100 C100+c00+w00 W101 C101+f101 W102 C102+h010 W103 C103+h011+g
-W010+f103 C110 W011 C111 W012+c01+c10+w10+f011 C112+h110 W013 C113+h111 W110+f013 N000 W111 N001
-W112+c11+w01+f111 N002 W113 N003 C020+f113 C021 C022 C023 C120 R000+r000 R001+r001 C121+c02+w11 R002+r002
-R003+r003 M100 M101 C122+y00 M102 M103 C123 M010 M011 M012+c12 M013 R100+r100 R101+r101 M110 M111 R102+r102
-Q103+r103 M112 M113+y10 R010+r010 R011+r011 M200 M201 R012+r012 Q013+r013 M202 M203+y01 R110+r110 R111+r111
-M210 M211 R112+r112 Q113+r113 M212 M213+y11 R200+r200 R201+r201 R202+r202 Q203+r203 Q210+r210+y20 Q211+r211
-Q212+r212 R213+r213 i i+y21
-"""
-LOADS = "p0 s e0 h00 x0 p1 h10 e1 x1 h01 h11 e2"
-LAG_W = 6
-LAG_ROUND = 6
-LAG_YQ = 12
+RUN = 4
 
 
 def tile_user_neighbour_rating_prediction_k4_kernel(
@@ -50,143 +38,130 @@ def tile_user_neighbour_rating_prediction_k4_kernel(
         def kept(name, shape, dtype):
             return keep.tile(shape, dtype, name=name, align_bytes=64)
 
+        def group(g):
+            return slice(g * GROUP, (g + 1) * GROUP)
+
+        def block(b):
+            return slice(b * P, (b + 1) * P)
+
         ident = kept("ident", [P, P], F32)
         e_plane = kept("e_plane", [P, JG, I], U8)
         x_plane = kept("x_plane", [P, U], U8)
-        zeros = None
         nc.vector.memset(e_plane[:].rearrange("p g n -> p (g n)").bitcast(I32), 0)
         nc.vector.memset(x_plane[:].bitcast(I32), 0)
         make_identity(nc, ident[:])
 
+        dev_sb = kept("dev_sb", [P, VG, SLOTS], BF16)
+        gain_raw = kept("gain_raw", [P, IG, SLOTS], BF16)
+        off_raw = kept("off_raw", [P, IG, SLOTS], BF16)
+        gain_sb = kept("gain_sb", [P, IG, SLOTS], F32)
+        off_sb = kept("off_sb", [P, IG, SLOTS], F32)
+        conf_row = kept("conf_row", [P, U], BF16)
         prof_sb, x_sb, e_sb, h_sb = {}, {}, {}, {}
 
         def load_prof(vg):
-            rows = prof[vg * GROUP : (vg + 1) * GROUP, :].rearrange("(m t) k -> m t k", t=PACK)
-            for t in range(PACK):
+            rows = prof[group(vg), :].rearrange("(m t) k -> m t k", t=SLOTS)
+            for t in range(SLOTS):
                 prof_sb[vg, t] = kept("prof_%d_%d" % (vg, t), [P, J], BF16)
                 nc.sync.dma_start(out=prof_sb[vg, t][:], in_=rows[:, t, :])
 
         def load_x(ug):
             x_sb[ug] = kept("x_%d" % ug, [P, JG, GROUP], U32)
-            src = x_words.rearrange("g p n t -> p g (n t)")[:, :, ug * GROUP * PACK : (ug + 1) * GROUP * PACK]
-            nc.sync.dma_start(out=x_sb[ug][:].bitcast(I32), in_=src.bitcast(I32))
+            words = x_words.rearrange("g p n t -> p g (n t)").bitcast(I32)
+            nc.sync.dma_start(out=x_sb[ug][:].bitcast(I32), in_=words[:, :, group(ug)])
 
         def load_e(ig):
             e_sb[ig] = kept("e_%d" % ig, [P, JG, 2 * GROUP], U8)
-            src = e_words.rearrange("g p b -> p g b")[:, :, ig * 2 * GROUP : (ig + 1) * 2 * GROUP]
+            src = e_words.rearrange("g p b -> p g b")[:, :, 2 * ig * GROUP : 2 * (ig + 1) * GROUP]
             nc.sync.dma_start(out=e_sb[ig][:].bitcast(I32), in_=src.bitcast(I32))
 
         def load_h(vg, ug):
-            h_sb[vg, ug] = kept("h_%d_%d" % (vg, ug), [P, PACK, GROUP], BF16)
-            rows = h[vg * GROUP : (vg + 1) * GROUP, ug * GROUP : (ug + 1) * GROUP]
-            nc.sync.dma_start(out=h_sb[vg, ug][:], in_=rows.rearrange("(p t) u -> p t u", t=PACK))
+            h_sb[vg, ug] = kept("h_%d_%d" % (vg, ug), [P, SLOTS, GROUP], BF16)
+            nc.sync.dma_start(out=h_sb[vg, ug][:], in_=h[group(vg), group(ug)].rearrange("(p t) u -> p t u", t=SLOTS))
 
-        dev_sb = kept("dev_sb", [P, VG, PACK], BF16)
-        gain_raw = kept("gain_raw", [P, IG, PACK], BF16)
-        off_raw = kept("off_raw", [P, IG, PACK], BF16)
-        conf_row = kept("conf_row", [P, U], BF16)
-        nc.gpsimd.dma_start(out=dev_sb[:], in_=dev.rearrange("(g p t) -> p g t", p=P, t=PACK))
-        for q in range(4):
-            nc.gpsimd.dma_start(
-                out=x_plane[32 * q : 32 * q + 4 * JG, :].bitcast(I32),
-                in_=x_scales[:, 4 * q : 4 * q + 4, :].bitcast(I32),
+        def scale_rows(q):
+            return slice(SCALE_ROWS * q, SCALE_ROWS * (q + 1))
+
+        def live_rows(q, planes):
+            return slice(QUADRANT * q, QUADRANT * q + SCALE_ROWS * planes)
+
+        nc.gpsimd.dma_start(out=dev_sb[:], in_=dev.rearrange("(g p t) -> p g t", p=P, t=SLOTS))
+        for q in range(QUADRANTS):
+            nc.gpsimd.dma_start(out=x_plane[live_rows(q, JG), :].bitcast(I32), in_=x_scales[:, scale_rows(q), :].bitcast(I32))
+        load_prof(0)
+        for q in range(QUADRANTS):
+            nc.sync.dma_start(
+                out=e_plane[live_rows(q, 1), :, :].bitcast(I32),
+                in_=e_scales[:, scale_rows(q), :].rearrange("g r n -> r g n").bitcast(I32),
             )
-
-        def load_s():
-            for q in range(4):
-                nc.sync.dma_start(
-                    out=e_plane[32 * q : 32 * q + 4, :, :].bitcast(I32),
-                    in_=e_scales[:, 4 * q : 4 * q + 4, :].rearrange("g r n -> r g n").bitcast(I32),
-                )
-
-        for tok in LOADS.split():
-            {"s": load_s, "e": load_e, "x": load_x, "h": load_h, "p": load_prof}[tok[0]](*[int(ch) for ch in tok[1:]])
-        nc.sync.dma_start(out=gain_raw[:], in_=gain.rearrange("(g p t) -> p g t", p=P, t=PACK))
-        nc.sync.dma_start(out=off_raw[:], in_=off.rearrange("(g p t) -> p g t", p=P, t=PACK))
+        load_e(0)
+        load_h(0, 0)
+        load_x(0)
+        load_prof(1)
+        load_h(1, 0)
+        load_e(1)
+        load_x(1)
+        load_h(0, 1)
+        load_h(1, 1)
+        load_e(2)
+        nc.sync.dma_start(out=gain_raw[:], in_=gain.rearrange("(g p t) -> p g t", p=P, t=SLOTS))
+        nc.sync.dma_start(out=off_raw[:], in_=off.rearrange("(g p t) -> p g t", p=P, t=SLOTS))
         nc.sync.dma_start(out=conf_row[:], in_=conf.partition_broadcast(P))
-
-        warm = kept("warm", [P, 1], F32)
-        nc.scalar.activation(out=warm[:], in_=ident[:, 0:1], func=ACT.Abs)
-
-        gain_f = kept("gain_f", [P, IG, PACK], F32)
-        off_f = kept("off_f", [P, IG, PACK], F32)
-        b_bf, b_codes, b_plane = {}, {}, {}
-        w_codes, w_plane, c_codes, c_plane = {}, {}, {}, {}
-        w_bf, c_bf, y_t, y_out = {}, {}, {}, {}
-        y_planes = [kept("y_plane_a", [P, U], U8), kept("y_plane_b", [P, U], U8)]
 
         later = {}
         clock = [0]
 
-        def after(lag, fn):
-            later.setdefault(clock[0] + lag, []).append(fn)
+        def after(steps, *call):
+            later.setdefault(clock[0] + steps, []).append(call)
 
-        quantizers = {}
+        def step(job, *followers):
+            for call in later.get(clock[0], []):
+                call[0](*call[1:])
+            job[0](*job[1:])
+            for call in followers:
+                after(1, *call)
+            clock[0] = clock[0] + 1
 
-        def quantize_next(*keys):
-            for key in keys:
-                later.setdefault(clock[0] + 1, []).append(quantizers[key])
+        def pause():
+            return None
 
         def next_bank():
-            return psum.tile([P, PACK, P], F32, name="bank", tag="bank%d" % (clock[0] % BANKS))
+            return psum.tile([P, SLOTS, P], F32, name="bank", tag="bank%d" % (clock[0] % BANKS))
 
         def quantize(codes, plane, src):
             nc.vector.quantize_mx(out=codes.bitcast(FP8X4), scales=plane, in_=src)
 
-        pair = [None, None]
-        h_words = {}
+        def interleave(copy, dst, src):
+            copy(out=dst.rearrange("p (c i) t -> p c t i", i=RUN), in_=src.rearrange("p t (c i) -> p c t i", i=RUN))
 
-        def interleave_h(vg, ug, half):
-            def run():
-                if half == 0:
-                    h_words[vg, ug] = work.tile([P, GROUP, PACK], BF16, name="h_words", bufs=3)
-                users = slice(half * 2 * P, (half + 1) * 2 * P)
-                nc.scalar.copy(
-                    out=h_words[vg, ug][:, users, :].rearrange("p (c i) t -> p c t i", i=4),
-                    in_=h_sb[vg, ug][:, :, users].rearrange("p t (c i) -> p c t i", i=4),
-                )
-
-            return run
-
-        for vg in range(VG):
-            for ug in range(UG):
-                for half in range(2):
-                    quantizers["h", vg, ug, half] = interleave_h(vg, ug, half)
+        b_bf = [kept("b_bf_%d" % vg, [P, SLOTS, JG * GROUP], BF16) for vg in range(VG)]
+        b_codes = [kept("b_codes_%d" % vg, [P, SLOTS, JG, P], U32) for vg in range(VG)]
+        b_plane = [kept("b_plane_%d" % vg, [P, SLOTS, JG, P], U8) for vg in range(VG)]
 
         def turn_prof(vg, t):
             bank = next_bank()
             words = prof_sb[vg, t][:].bitcast(F32)
             for jg in range(JG):
                 for e in range(2):
-                    nc.tensor.transpose(bank[:, 2 * jg + e, :], words[:, 256 * jg + e : 256 * (jg + 1) : 2], ident[:])
-            if t == 0:
-                b_bf[vg] = kept("b_bf_%d" % vg, [P, PACK, JG * GROUP], BF16)
-                b_codes[vg] = kept("b_codes_%d" % vg, [P, PACK, JG, P], U32)
-                b_plane[vg] = kept("b_plane_%d" % vg, [P, PACK, JG, P], U8)
+                    nc.tensor.transpose(bank[:, 2 * jg + e, :], words[:, 2 * P * jg + e : 2 * P * (jg + 1) : 2], ident[:])
+            after(1, pair_words, bank, vg, t)
 
-            def leave():
-                nc.scalar.copy(
-                    out=b_bf[vg][:, t, :].bitcast(F32).rearrange("p (g m e) -> p g m e", g=JG, e=2),
-                    in_=bank[:].rearrange("p (g e) m -> p g m e", e=2),
-                )
+        def pair_words(bank, vg, t):
+            nc.scalar.copy(
+                out=b_bf[vg][:, t, :].bitcast(F32).rearrange("p (g m e) -> p g m e", g=JG, e=2),
+                in_=bank[:].rearrange("p (g e) m -> p g m e", e=2),
+            )
 
-            def quant(first):
-                def run():
-                    quantize(
-                        b_codes[vg][:, first : t + 1].rearrange("p t g m -> p (t g m)"),
-                        b_plane[vg][:, first : t + 1].rearrange("p t g m -> p (t g m)"),
-                        b_bf[vg][:, first : t + 1].rearrange("p t k -> p (t k)"),
-                    )
-
-                return run
-
-            after(1, leave)
-            quantizers["b", vg, t] = quant(t)
-            quantizers["B", vg] = quant(0)
+        def quantize_b(vg, first, last):
+            quantize(
+                b_codes[vg][:, first : last + 1].rearrange("p t g m -> p (t g m)"),
+                b_plane[vg][:, first : last + 1].rearrange("p t g m -> p (t g m)"),
+                b_bf[vg][:, first : last + 1].rearrange("p t k -> p (t k)"),
+            )
 
         def first_stage(vg, moving, planes):
             bank = next_bank()
-            for t in range(PACK):
+            for t in range(SLOTS):
                 for jg in range(JG):
                     nc.tensor.matmul_mx(
                         out=bank[:, t, :],
@@ -199,82 +174,96 @@ def tile_user_neighbour_rating_prediction_k4_kernel(
                     )
             return bank
 
-        def w_chunk(vg, ug, c):
-            cols = slice(c * P, (c + 1) * P)
-            u0 = ug * GROUP + c * P
+        h_words, w_factors, w_bf, w_codes, w_plane = {}, {}, {}, {}, {}
+
+        def order_h(vg, ug, pair):
+            if pair == 0:
+                h_words[vg, ug] = work.tile([P, GROUP, SLOTS], BF16, name="h_words")
+            users = slice(2 * P * pair, 2 * P * (pair + 1))
+            interleave(nc.scalar.copy, h_words[vg, ug][:, users, :], h_sb[vg, ug][:, :, users])
+
+        def w_block(vg, ug, b):
+            u0 = ug * GROUP + b * P
             bank = first_stage(
                 vg,
-                [x_sb[ug][:, jg, cols].bitcast(FP8X4) for jg in range(JG)],
-                [x_plane[4 * jg : P, u0 : u0 + P] for jg in range(JG)],
+                [x_sb[ug][:, jg, block(b)].bitcast(FP8X4) for jg in range(JG)],
+                [x_plane[SCALE_ROWS * jg : P, u0 : u0 + P] for jg in range(JG)],
             )
-            if c % 2 == 0:
-                pair[0] = work.tile([P, 2 * P, PACK], F32, name="cos_h", bufs=3)
-                pair[1] = work.tile([P, 2 * P, PACK], F32, name="size", bufs=3)
-            cos_h, size = pair
-            half = slice((c % 2) * P, (c % 2 + 1) * P)
-            by_column = bank[:].rearrange("p t u -> p u t")
+            if b % 2 == 0:
+                cos_h = work.tile([P, 2 * P, SLOTS], F32, name="cos_h")
+                cos_abs = work.tile([P, 2 * P, SLOTS], F32, name="cos_abs")
+                w_factors[vg, ug, b // 2] = (cos_h, cos_abs)
+            after(1, shrink, bank, vg, ug, b)
+            after(2, magnitude, bank, vg, ug, b)
 
-            def shrink():
-                nc.vector.tensor_tensor(out=cos_h[:, half, :], in0=by_column, in1=h_words[vg, ug][:, cols, :], op=ALU.mult)
+        def shrink(bank, vg, ug, b):
+            nc.vector.tensor_tensor(
+                out=w_factors[vg, ug, b // 2][0][:, block(b % 2), :],
+                in0=bank[:].rearrange("p t u -> p u t"),
+                in1=h_words[vg, ug][:, block(b), :],
+                op=ALU.mult,
+            )
 
-            def magnitude():
-                nc.scalar.activation(out=size[:, half, :], in_=by_column, func=ACT.Abs)
+        def magnitude(bank, vg, ug, b):
+            nc.scalar.activation(
+                out=w_factors[vg, ug, b // 2][1][:, block(b % 2), :], in_=bank[:].rearrange("p t u -> p u t"), func=ACT.Abs
+            )
 
-            def weigh():
-                if c == 1:
-                    w_bf[vg, ug] = work.tile([P, GROUP, PACK], BF16, name="w_bf", align_bytes=64, bufs=1)
-                dst = w_bf[vg, ug]
-                nc.gpsimd.tensor_tensor(out=dst[:, (c - 1) * P : (c + 1) * P, :], in0=cos_h[:], in1=size[:], op=ALU.mult)
+        def finish_w(vg, ug, pair):
+            if pair == 0:
+                w_bf[vg, ug] = work.tile([P, GROUP, SLOTS], BF16, name="w_bf", align_bytes=64, bufs=1)
+            cos_h, cos_abs = w_factors[vg, ug, pair]
+            users = slice(2 * P * pair, 2 * P * (pair + 1))
+            nc.gpsimd.tensor_tensor(out=w_bf[vg, ug][:, users, :], in0=cos_h[:], in1=cos_abs[:], op=ALU.mult)
 
-            def quant():
-                w_codes[vg, ug] = kept("w_codes_%d_%d" % (vg, ug), [P, GROUP], U32)
-                w_plane[vg, ug] = kept("w_plane_%d_%d" % (vg, ug), [P, GROUP], U8)
-                quantize(w_codes[vg, ug][:], w_plane[vg, ug][:], w_bf[vg, ug][:].rearrange("p u t -> p (u t)"))
+        def quantize_w(vg, ug):
+            w_codes[vg, ug] = kept("w_codes_%d_%d" % (vg, ug), [P, GROUP], U32)
+            w_plane[vg, ug] = kept("w_plane_%d_%d" % (vg, ug), [P, GROUP], U8)
+            quantize(w_codes[vg, ug][:], w_plane[vg, ug][:], w_bf[vg, ug][:].rearrange("p u t -> p (u t)"))
 
-            after(1, shrink)
-            after(2, magnitude)
-            if c % 2 == 1:
-                quantizers["f", vg, ug, c] = weigh
-            if c == PACK - 1:
-                quantizers["w", vg, ug] = quant
+        c_bf, c_codes, c_plane = {}, {}, {}
+        per_block = P // SLOTS
 
-        def c_chunk(vg, ig, c):
-            i0 = ig * GROUP + c * P
+        def c_block(vg, ig, b):
+            i0 = ig * GROUP + b * P
             bank = first_stage(
                 vg,
-                [e_sb[ig][:, jg, 2 * c * P : 2 * (c + 1) * P].bitcast(FP4X4) for jg in range(JG)],
+                [e_sb[ig][:, jg, 2 * b * P : 2 * (b + 1) * P].bitcast(FP4X4) for jg in range(JG)],
                 [e_plane[:, jg, i0 : i0 + P] for jg in range(JG)],
             )
-            if c == 0:
-                c_bf[vg, ig] = work.tile([P, PACK, P, PACK], BF16, name="c_bf", align_bytes=64, bufs=3)
-            dst = c_bf[vg, ig]
+            if b == 0:
+                c_bf[vg, ig] = work.tile([P, SLOTS, P, SLOTS], BF16, name="c_bf", align_bytes=64)
+            after(1, scale_c, bank, vg, ig, b)
 
-            def scale():
-                nc.vector.tensor_tensor(
-                    out=dst[:, :, 32 * c : 32 * (c + 1), :].rearrange("p s m t -> p m s t"),
-                    in0=bank[:].rearrange("p t (m s) -> p m s t", s=PACK),
-                    in1=dev_sb[:, vg, :].rearrange("p (a b t) -> p a b t", a=1, b=1).to_broadcast([P, 32, PACK, PACK]),
-                    op=ALU.mult,
-                )
+        def scale_c(bank, vg, ig, b):
+            dev_slots = dev_sb[:, vg, :].rearrange("p (m s t) -> p m s t", m=1, s=1)
+            nc.vector.tensor_tensor(
+                out=c_bf[vg, ig][:, :, per_block * b : per_block * (b + 1), :].rearrange("p s m t -> p m s t"),
+                in0=bank[:].rearrange("p t (m s) -> p m s t", s=SLOTS),
+                in1=dev_slots.to_broadcast([P, per_block, SLOTS, SLOTS]),
+                op=ALU.mult,
+            )
 
-            def quant():
-                c_codes[vg, ig] = kept("c_codes_%d_%d" % (vg, ig), [P, GROUP], U32)
-                c_plane[vg, ig] = kept("c_plane_%d_%d" % (vg, ig), [P, GROUP], U8)
-                quantize(c_codes[vg, ig][:], c_plane[vg, ig][:], dst[:].rearrange("p s m t -> p (s m t)"))
+        def quantize_c(vg, ig):
+            c_codes[vg, ig] = kept("c_codes_%d_%d" % (vg, ig), [P, GROUP], U32)
+            c_plane[vg, ig] = kept("c_plane_%d_%d" % (vg, ig), [P, GROUP], U8)
+            quantize(c_codes[vg, ig][:], c_plane[vg, ig][:], c_bf[vg, ig][:].rearrange("p s m t -> p (s m t)"))
 
-            after(1, scale)
-            if c == PACK - 1:
-                quantizers["c", vg, ig] = quant
+        y_t, y_bf, y_codes = {}, {}, {}
+        y_planes = [kept("y_plane_a", [P, U], U8), kept("y_plane_b", [P, U], U8)]
 
-        def second_stage(ig, ug, s, on_scalar):
-            bank = next_bank()
-            flat = bank[:].rearrange("p a b -> p (a b)")
-            cols = slice(s * P, (s + 1) * P)
+        def widen_gain_off():
+            nc.scalar.copy(out=gain_sb[:], in_=gain_raw[:])
+            nc.scalar.copy(out=off_sb[:], in_=off_raw[:])
+
+        def predict(unit, s, by_item):
+            ig, ug = unit
+            bank = next_bank()[:].rearrange("p a b -> p (a b)")
             for vg in range(VG):
                 nc.tensor.matmul_mx(
-                    out=flat,
-                    lhsT=c_codes[vg, ig][:, cols].bitcast(FP8X4),
-                    lhsT_scale=c_plane[vg, ig][:, cols],
+                    out=bank,
+                    lhsT=c_codes[vg, ig][:, block(s)].bitcast(FP8X4),
+                    lhsT_scale=c_plane[vg, ig][:, block(s)],
                     rhs=w_codes[vg, ug][:].bitcast(FP8X4),
                     rhs_scale=w_plane[vg, ug][:],
                     start=(vg == 0),
@@ -282,171 +271,167 @@ def tile_user_neighbour_rating_prediction_k4_kernel(
                 )
             p_conf = work.tile([P, GROUP], F32, name="p_conf", bufs=4)
             if s == 0:
-                y_t[ig, ug] = work.tile([P, PACK, GROUP], F32, name="y_t", bufs=3)
-            dst = y_t[ig, ug]
+                y_t[unit] = work.tile([P, SLOTS, GROUP], F32, name="y_t")
+            after(1, by_user, bank, p_conf, ug)
+            after(2, by_item, p_conf, unit, s)
 
-            def by_user():
-                nc.vector.tensor_tensor(out=p_conf[:], in0=flat, in1=conf_row[:, ug * GROUP : (ug + 1) * GROUP], op=ALU.mult)
+        def by_user(bank, p_conf, ug):
+            nc.vector.tensor_tensor(out=p_conf[:], in0=bank, in1=conf_row[:, group(ug)], op=ALU.mult)
 
-            def by_item():
-                if on_scalar:
-                    nc.scalar.activation(
-                        out=dst[:, s, :],
-                        in_=p_conf[:],
-                        func=ACT.Identity,
-                        scale=gain_f[:, ig, s : s + 1],
-                        bias=off_f[:, ig, s : s + 1],
-                    )
-                    return
-                nc.gpsimd.tensor_scalar(
-                    out=dst[:, s, :],
-                    in0=p_conf[:],
-                    scalar1=gain_f[:, ig, s : s + 1],
-                    scalar2=off_f[:, ig, s : s + 1],
-                    op0=ALU.mult,
-                    op1=ALU.add,
+        def by_item_on_scalar(p_conf, unit, s):
+            nc.scalar.activation(
+                out=y_t[unit][:, s, :],
+                in_=p_conf[:],
+                func=ACT.Identity,
+                scale=gain_sb[:, unit[0], s : s + 1],
+                bias=off_sb[:, unit[0], s : s + 1],
+            )
+
+        def by_item_on_gpsimd(p_conf, unit, s):
+            nc.gpsimd.tensor_scalar(
+                out=y_t[unit][:, s, :],
+                in0=p_conf[:],
+                scalar1=gain_sb[:, unit[0], s : s + 1],
+                scalar2=off_sb[:, unit[0], s : s + 1],
+                op0=ALU.mult,
+                op1=ALU.add,
+            )
+
+        def turn_y(unit, b, copy):
+            bank = next_bank()
+            for s in range(SLOTS):
+                nc.tensor.transpose(bank[:, s, :], y_t[unit][:, s, block(b)], ident[:])
+            y_rows = work.tile([P, GROUP], F32, name="y_rows", bufs=6)
+            after(1, store_y, bank, y_rows, unit, b, copy)
+
+        def store_y(bank, y_rows, unit, b, copy):
+            ig, ug = unit
+            copy(out=y_rows[:].rearrange("p (m s) -> p m s", s=SLOTS), in_=bank[:].rearrange("p s m -> p m s"))
+            u0 = ug * GROUP + b * P
+            nc.sync.dma_start(out=out_0[u0 : u0 + P, group(ig)], in_=y_rows[:])
+
+        def round_y(unit, b, copy):
+            if unit not in y_bf:
+                y_bf[unit] = work.tile([P, GROUP, SLOTS], BF16, name="y_bf", align_bytes=64)
+            interleave(copy, y_bf[unit][:, block(b), :], y_t[unit][:, :, block(b)])
+
+        def quantize_y(unit):
+            ig, ug = unit
+            y_codes[unit] = work.tile([P, GROUP], U32, name="y_codes", align_bytes=64)
+            plane = y_planes[ig // 2][SCALE_ROWS * (ig % 2) : P, group(ug)]
+            quantize(y_codes[unit][:], plane, y_bf[unit][:].rearrange("p u t -> p (u t)"))
+
+        def store_codes(unit):
+            ig, ug = unit
+            words = out_1[ig].rearrange("p m t -> p (m t)").bitcast(I32)
+            nc.sync.dma_start(out=words[:, group(ug)], in_=y_codes[unit][:].bitcast(I32))
+
+        def store_planes(first, count):
+            for q in range(QUADRANTS):
+                nc.sync.dma_start(
+                    out=out_2[first : first + count, scale_rows(q), :].bitcast(I32),
+                    in_=y_planes[first // 2][live_rows(q, count), :].bitcast(I32),
                 )
 
-            y_bf = []
+        on_scalar, on_vector = nc.scalar.copy, nc.vector.tensor_copy
 
-            def round_y(ub):
-                def run():
-                    if ub == 0:
-                        y_bf.append(work.tile([P, GROUP, PACK], BF16, name="y_bf", align_bytes=64, bufs=3))
-                    users = slice(ub * P, (ub + 1) * P)
-                    nc.scalar.copy(
-                        out=y_bf[0][:, users, :].rearrange("p (c i) t -> p c t i", i=4),
-                        in_=dst[:, :, users].rearrange("p t (c i) -> p c t i", i=4),
-                    )
+        def weave(first, second, followers):
+            jobs = [job for both in zip(first, second) for job in both]
+            for n, job in enumerate(jobs):
+                step(job, *followers.get(n, []))
 
-                return run
+        def w_blocks(vg, ug):
+            return [(w_block, vg, ug, b) for b in range(SLOTS)]
 
-            def quant():
-                y_codes = work.tile([P, GROUP], U32, name="y_codes", align_bytes=64, bufs=2)
-                row = 4 * (ig % 2)
-                plane = y_planes[ig // 2]
-                quantize(y_codes[:], plane[row:P, ug * GROUP : (ug + 1) * GROUP], y_bf[0][:].rearrange("p u t -> p (u t)"))
-                words = out_1[ig].rearrange("p m t -> p (m t)")[:, ug * GROUP * PACK : (ug + 1) * GROUP * PACK]
-                nc.sync.dma_start(out=words.bitcast(I32), in_=y_codes[:].bitcast(I32))
-                if ug == UG - 1 and ig >= 1:
-                    first = 2 * (ig // 2)
-                    for q in range(4):
-                        nc.sync.dma_start(
-                            out=out_2[first : ig + 1, 4 * q : 4 * q + 4, :].bitcast(I32),
-                            in_=plane[32 * q : 32 * q + row + 4, :].bitcast(I32),
-                        )
+        def c_blocks(vg, ig):
+            return [(c_block, vg, ig, b) for b in range(SLOTS)]
 
-            after(1, by_user)
-            after(2, by_item)
-            if s == PACK - 1:
-                for ub in range(PACK):
-                    quantizers["r", ig, ug, ub] = round_y(ub)
-                quantizers["y", ig, ug] = quant
+        step((turn_prof, 0, 0))
+        for t in range(1, SLOTS):
+            step((turn_prof, 0, t), (quantize_b, 0, t - 1, t - 1))
+        step((pause,), (quantize_b, 0, SLOTS - 1, SLOTS - 1), (order_h, 0, 0, 0), (order_h, 0, 0, 1))
+        step((pause,))
 
-        def turn_y(ig, ug, ub, on_vector):
-            bank = next_bank()
-            for s in range(PACK):
-                nc.tensor.transpose(bank[:, s, :], y_t[ig, ug][:, s, ub * P : (ub + 1) * P], ident[:])
-            if ub % 2 == 0:
-                y_out[ig, ug] = work.tile([P, 2, GROUP], F32, name="y_out", bufs=5)
-            dst = y_out[ig, ug]
+        weave(c_blocks(0, 0)[:3], w_blocks(0, 0)[:3], {})
+        step((turn_prof, 1, 0), (finish_w, 0, 0, 0))
+        step((turn_prof, 1, 1))
+        step((c_block, 0, 0, 3))
+        step((turn_prof, 1, 2))
+        step((turn_prof, 1, 3), (quantize_c, 0, 0))
+        step((w_block, 0, 0, 3), (quantize_b, 1, 0, SLOTS - 1), (order_h, 1, 0, 0))
+        step((c_block, 0, 1, 0), (order_h, 1, 0, 1))
+        step((c_block, 0, 1, 1), (finish_w, 0, 0, 1))
+        step((c_block, 0, 1, 2))
+        step((c_block, 0, 1, 3))
 
-            def leave():
-                rows = dst[:, ub % 2, :].rearrange("p (m s) -> p m s", s=PACK)
-                src = bank[:].rearrange("p s m -> p m s")
-                if on_vector:
-                    nc.vector.tensor_copy(out=rows, in_=src)
-                else:
-                    nc.scalar.copy(out=rows, in_=src)
-                if ub % 2 == 1:
-                    u0 = ug * GROUP + (ub - 1) * P
-                    block = out_0[u0 : u0 + 2 * P, ig * GROUP : (ig + 1) * GROUP]
-                    nc.sync.dma_start(out=block.rearrange("(b p) i -> p b i", p=P), in_=dst[:])
+        weave(
+            w_blocks(1, 0),
+            c_blocks(1, 0),
+            {
+                1: [(order_h, 0, 1, 0)],
+                4: [(quantize_w, 0, 0), (quantize_c, 0, 1), (finish_w, 1, 0, 0)],
+                5: [(order_h, 0, 1, 1)],
+                7: [(widen_gain_off,)],
+            },
+        )
+        weave(
+            w_blocks(0, 1),
+            c_blocks(1, 1),
+            {
+                0: [(finish_w, 1, 0, 1)],
+                1: [(order_h, 1, 1, 0)],
+                4: [(quantize_w, 1, 0), (quantize_c, 1, 0), (finish_w, 0, 1, 0)],
+                5: [(order_h, 1, 1, 1)],
+            },
+        )
+        weave(
+            w_blocks(1, 1),
+            [(predict, (0, 0), s, by_item_on_scalar) for s in range(SLOTS)],
+            {0: [(finish_w, 0, 1, 1)], 4: [(quantize_c, 1, 1), (quantize_w, 0, 1), (finish_w, 1, 1, 0)]},
+        )
 
-            after(1, leave)
+        step((predict, (1, 0), 0, by_item_on_scalar), (finish_w, 1, 1, 1))
+        step((predict, (1, 0), 1, by_item_on_scalar))
+        step((c_block, 0, 2, 0))
+        step((c_block, 0, 2, 1))
+        for b in (0, 1):
+            step((turn_y, (0, 0), b, on_scalar), (round_y, (0, 0), b, on_scalar))
+        step((predict, (1, 0), 2, by_item_on_scalar))
+        step((predict, (1, 0), 3, by_item_on_gpsimd), (quantize_w, 1, 1))
+        step((c_block, 0, 2, 2))
+        step((c_block, 0, 2, 3))
+        for b in (2, 3):
+            step((turn_y, (0, 0), b, on_scalar), (round_y, (0, 0), b, on_scalar))
+        step((c_block, 1, 2, 0), (quantize_c, 0, 2))
+        step((c_block, 1, 2, 1))
 
-        def weave(a, b):
-            merged = []
-            for k in range(max(len(a), len(b))):
-                merged.extend(a[k : k + 1])
-                merged.extend(b[k : k + 1])
-            return merged
+        units = [(0, 0), (1, 0), (0, 1), (1, 1), (2, 0), (2, 1)]
+        for n in range(2, len(units)):
+            unit, before, oldest = units[n], units[n - 1], units[n - 2]
+            last = n == len(units) - 1
+            step(
+                (predict, unit, 0, by_item_on_gpsimd),
+                (quantize_y, oldest),
+                (round_y, before, 2, on_vector),
+                (round_y, before, 3, on_vector),
+            )
+            stores = [(store_codes, oldest)] + ([(store_planes, 0, 2)] if last else [])
+            step((predict, unit, 1, by_item_on_gpsimd), *stores)
+            for b in (0, 1):
+                step((turn_y, before, b, on_scalar), (round_y, before, b, on_scalar))
+            step((predict, unit, 2, by_item_on_gpsimd))
+            step((predict, unit, 3, by_item_on_scalar))
+            if n == 2:
+                step((c_block, 1, 2, 2))
+                step((c_block, 1, 2, 3))
+            copy = on_vector if last else on_scalar
+            step((turn_y, before, 2, copy))
+            closing = [(quantize_c, 1, 2)] if n == 2 else [(quantize_y, before)] if last else []
+            step((turn_y, before, 3, copy), *closing)
 
-        def t_jobs(vg):
-            return [(turn_prof, vg, t) for t in range(PACK)]
-
-        def w_jobs(vg, ug):
-            return [(w_chunk, vg, ug, c) for c in range(PACK)]
-
-        def c_jobs(vg, ig):
-            return [(c_chunk, vg, ig, c) for c in range(PACK)]
-
-        def m_jobs(ig, ug, n_scalar):
-            return [(second_stage, ig, ug, s, s >= PACK - n_scalar) for s in range(PACK)]
-
-        def widen():
-            nc.scalar.copy(out=gain_f[:], in_=gain_raw[:])
-            nc.scalar.copy(out=off_f[:], in_=off_raw[:])
-
-        def then(job, *keys):
-            def run():
-                job[0](*job[1:])
-                quantize_next(*keys)
-
-            return (run,)
-
-        def closing(jobs, *keys):
-            return jobs[:-1] + [then(jobs[-1], *keys)]
-
-        def rounding(jobs, ig, ug):
-            return [then(job, ("r", ig, ug, ub)) for ub, job in enumerate(jobs[:PACK])] + jobs[PACK:]
-
-        def opening(jobs, *keys):
-            return [then(jobs[0], *keys)] + jobs[1:]
-
-        def r_jobs(ig, ug, n_vector):
-            return [(turn_y, ig, ug, ub, ub < n_vector) for ub in range(PACK)]
-
-        def warm_up(n):
-            bank = next_bank()
-            for k in range(n):
-                nc.tensor.matmul(bank[:].rearrange("p a b -> p (a b)"), lhsT=zeros[:, :P], rhs=zeros[:], start=True, stop=True)
-
-        def idle():
-            return None
-
-        wait = [(idle,)]
-        def triples(cs, ws):
-            merged = []
-            for k in range(len(ws)):
-                merged.extend(cs[2 * k : 2 * k + 1] + ws[k : k + 1] + cs[2 * k + 1 : 2 * k + 2])
-            return merged
-
-        jobs = []
-        for tok in ORDER.split():
-            parts = tok.split("+")
-            kind, d = parts[0][0], [int(ch) for ch in parts[0][1:]]
-            if kind == "T":
-                job = (turn_prof, d[0], d[1])
-            elif kind == "W":
-                job = (w_chunk, d[0], d[1], d[2])
-            elif kind == "C":
-                job = (c_chunk, d[0], d[1], d[2])
-            elif kind == "M" or kind == "N":
-                job = (second_stage, d[0], d[1], d[2], kind == "N")
-            elif kind == "R" or kind == "Q":
-                job = (turn_y, d[0], d[1], d[2], kind == "Q")
-            elif kind == "D":
-                job = (warm_up, d[0])
-            else:
-                job = (idle,)
-            keys = [tuple([p[0]] + [int(ch) for ch in p[1:]]) for p in parts[1:]]
-            jobs.append(then(job, *keys))
-        quantizers["g",] = widen
-        jobs = jobs + wait * 6
-
-        for job in jobs:
-            for fn in later.get(clock[0], []):
-                fn()
-            job[0](*job[1:])
-            clock[0] = clock[0] + 1
+        unit, before = units[-1], units[-2]
+        step((turn_y, unit, 0, on_scalar), (store_codes, before), (round_y, unit, 0, on_vector), (round_y, unit, 1, on_vector))
+        step((turn_y, unit, 1, on_scalar), (round_y, unit, 2, on_vector), (round_y, unit, 3, on_vector))
+        step((turn_y, unit, 2, on_scalar), (quantize_y, unit))
+        step((turn_y, unit, 3, on_scalar), (store_codes, unit), (store_planes, 2, 1))
+        step((pause,))

@@ -59,9 +59,9 @@ def tile_user_neighbour_rating_prediction_k4_kernel(
         conf_row = kept("conf_row", [P, U], BF16)
         prof_sb, x_sb, e_sb, h_sb = {}, {}, {}, {}
 
-        def load_prof(vg):
+        def load_prof(vg, slots):
             rows = prof[group(vg), :].rearrange("(m t) k -> m t k", t=SLOTS)
-            for t in range(SLOTS):
+            for t in slots:
                 prof_sb[vg, t] = kept("prof_%d_%d" % (vg, t), [P, J], BF16)
                 nc.sync.dma_start(out=prof_sb[vg, t][:], in_=rows[:, t, :])
 
@@ -85,19 +85,20 @@ def tile_user_neighbour_rating_prediction_k4_kernel(
         def live_rows(q, planes):
             return slice(QUADRANT * q, QUADRANT * q + SCALE_ROWS * planes)
 
-        nc.gpsimd.dma_start(out=dev_sb[:], in_=dev.rearrange("(g p t) -> p g t", p=P, t=SLOTS))
-        for q in range(QUADRANTS):
-            nc.gpsimd.dma_start(out=x_plane[live_rows(q, JG), :].bitcast(I32), in_=x_scales[:, scale_rows(q), :].bitcast(I32))
-        load_prof(0)
+        load_prof(0, (0, 1))
         for q in range(QUADRANTS):
             nc.sync.dma_start(
                 out=e_plane[live_rows(q, 1), :, :].bitcast(I32),
                 in_=e_scales[:, scale_rows(q), :].rearrange("g r n -> r g n").bitcast(I32),
             )
+        load_prof(0, (2, 3))
+        nc.sync.dma_start(out=dev_sb[:], in_=dev.rearrange("(g p t) -> p g t", p=P, t=SLOTS))
         load_e(0)
         load_h(0, 0)
         load_x(0)
-        load_prof(1)
+        for q in range(QUADRANTS):
+            nc.sync.dma_start(out=x_plane[live_rows(q, JG), :].bitcast(I32), in_=x_scales[:, scale_rows(q), :].bitcast(I32))
+        load_prof(1, range(SLOTS))
         load_h(1, 0)
         load_e(1)
         load_x(1)

@@ -132,8 +132,10 @@ def tile_user_neighbour_rating_prediction_k4_kernel(
         def quantize(codes, plane, src):
             nc.vector.quantize_mx(out=codes.bitcast(FP8X4), scales=plane, in_=src)
 
-        def interleave(copy, dst, src):
-            copy(out=dst.rearrange("p (c i) t -> p c t i", i=RUN), in_=src.rearrange("p t (c i) -> p c t i", i=RUN))
+        def interleave(dst, src):
+            nc.scalar.copy(
+                out=dst.rearrange("p (c i) t -> p c t i", i=RUN), in_=src.rearrange("p t (c i) -> p c t i", i=RUN)
+            )
 
         b_bf = [kept("b_bf_%d" % vg, [P, SLOTS, JG * GROUP], BF16) for vg in range(VG)]
         b_codes = [kept("b_codes_%d" % vg, [P, SLOTS, JG, P], U32) for vg in range(VG)]
@@ -181,7 +183,7 @@ def tile_user_neighbour_rating_prediction_k4_kernel(
             if pair == 0:
                 h_words[vg, ug] = work.tile([P, GROUP, SLOTS], BF16, name="h_words")
             users = slice(2 * P * pair, 2 * P * (pair + 1))
-            interleave(nc.scalar.copy, h_words[vg, ug][:, users, :], h_sb[vg, ug][:, :, users])
+            interleave(h_words[vg, ug][:, users, :], h_sb[vg, ug][:, :, users])
 
         def w_block(vg, ug, b):
             u0 = ug * GROUP + b * P
@@ -311,10 +313,10 @@ def tile_user_neighbour_rating_prediction_k4_kernel(
             u0 = ug * GROUP + b * P
             nc.sync.dma_start(out=out_0[u0 : u0 + P, group(ig)], in_=y_rows[:])
 
-        def round_y(unit, b, copy):
+        def round_y(unit, b):
             if unit not in y_bf:
                 y_bf[unit] = work.tile([P, GROUP, SLOTS], BF16, name="y_bf", align_bytes=64)
-            interleave(copy, y_bf[unit][:, block(b), :], y_t[unit][:, :, block(b)])
+            interleave(y_bf[unit][:, block(b), :], y_t[unit][:, :, block(b)])
 
         def quantize_y(unit):
             ig, ug = unit
@@ -391,48 +393,44 @@ def tile_user_neighbour_rating_prediction_k4_kernel(
             {0: [(finish_w, 0, 1, 1)], 4: [(quantize_c, 1, 1), (quantize_w, 0, 1), (finish_w, 1, 1, 0)]},
         )
 
-        step((predict, (1, 0), 0, by_item_on_scalar), (finish_w, 1, 1, 1))
-        step((predict, (1, 0), 1, by_item_on_scalar))
+        step((predict, (1, 0), 0, by_item_on_scalar), (finish_w, 1, 1, 1), (round_y, (0, 0), 0))
+        step((predict, (1, 0), 1, by_item_on_scalar), (round_y, (0, 0), 1))
         step((c_block, 0, 2, 0))
         step((c_block, 0, 2, 1))
-        for b in (0, 1):
-            step((turn_y, (0, 0), b, on_scalar), (round_y, (0, 0), b, on_scalar))
-        step((predict, (1, 0), 2, by_item_on_scalar))
-        step((predict, (1, 0), 3, by_item_on_gpsimd), (quantize_w, 1, 1))
+        step((turn_y, (0, 0), 0, on_scalar))
+        step((turn_y, (0, 0), 1, on_scalar))
+        step((predict, (1, 0), 2, by_item_on_scalar), (round_y, (0, 0), 2))
+        step((predict, (1, 0), 3, by_item_on_gpsimd), (quantize_w, 1, 1), (round_y, (0, 0), 3))
         step((c_block, 0, 2, 2))
         step((c_block, 0, 2, 3))
-        for b in (2, 3):
-            step((turn_y, (0, 0), b, on_scalar), (round_y, (0, 0), b, on_scalar))
+        step((turn_y, (0, 0), 2, on_scalar))
+        step((turn_y, (0, 0), 3, on_scalar))
         step((c_block, 1, 2, 0), (quantize_c, 0, 2))
         step((c_block, 1, 2, 1))
 
         units = [(0, 0), (1, 0), (0, 1), (1, 1), (2, 0), (2, 1)]
         for n in range(2, len(units)):
             unit, before, oldest = units[n], units[n - 1], units[n - 2]
-            last = n == len(units) - 1
-            step(
-                (predict, unit, 0, by_item_on_gpsimd),
-                (quantize_y, oldest),
-                (round_y, before, 2, on_vector),
-                (round_y, before, 3, on_vector),
-            )
-            stores = [(store_codes, oldest)] + ([(store_planes, 0, 2)] if last else [])
-            step((predict, unit, 1, by_item_on_gpsimd), *stores)
-            for b in (0, 1):
-                step((turn_y, before, b, on_scalar), (round_y, before, b, on_scalar))
-            step((predict, unit, 2, by_item_on_gpsimd))
-            step((predict, unit, 3, by_item_on_scalar))
-            if n == 2:
+            with_c, last = n == 2, n == len(units) - 1
+            stores = [(store_codes, oldest)] + ([(store_planes, 0, 2)] if oldest == (1, 1) else [])
+            step((predict, unit, 0, by_item_on_gpsimd), (quantize_y, oldest), (round_y, before, 0))
+            step((predict, unit, 1, by_item_on_gpsimd), *stores, (round_y, before, 1))
+            step((turn_y, before, 0, on_scalar))
+            step((turn_y, before, 1, on_scalar))
+            step((predict, unit, 2, by_item_on_gpsimd), (round_y, before, 2))
+            step((predict, unit, 3, by_item_on_scalar), (round_y, before, 3))
+            if with_c:
                 step((c_block, 1, 2, 2))
                 step((c_block, 1, 2, 3))
-            copy = on_vector if last else on_scalar
-            step((turn_y, before, 2, copy))
-            closing = [(quantize_c, 1, 2)] if n == 2 else [(quantize_y, before)] if last else []
-            step((turn_y, before, 3, copy), *closing)
+                step((turn_y, before, 2, on_scalar))
+                step((turn_y, before, 3, on_scalar), (quantize_c, 1, 2))
+            else:
+                step((turn_y, before, 2, on_vector))
+                step((turn_y, before, 3, on_vector), *([(round_y, unit, 0)] if last else []))
 
         unit, before = units[-1], units[-2]
-        step((turn_y, unit, 0, on_scalar), (store_codes, before), (round_y, unit, 0, on_vector), (round_y, unit, 1, on_vector))
-        step((turn_y, unit, 1, on_scalar), (round_y, unit, 2, on_vector), (round_y, unit, 3, on_vector))
-        step((turn_y, unit, 2, on_scalar), (quantize_y, unit))
-        step((turn_y, unit, 3, on_scalar), (store_codes, unit), (store_planes, 2, 1))
+        step((turn_y, unit, 0, on_scalar), (quantize_y, before), (round_y, unit, 1))
+        step((turn_y, unit, 1, on_vector), (store_codes, before), (round_y, unit, 2))
+        step((turn_y, unit, 2, on_vector), (round_y, unit, 3))
+        step((turn_y, unit, 3, on_vector), (quantize_y, unit), (store_codes, unit), (store_planes, 2, 1))
         step((pause,))

from contextlib import ExitStack

import concourse.mybir as mybir
from concourse.masks import make_identity

U, V, J, I = 1024, 1024, 1024, 1536
FLOPS = 2 * V * J * U + 2 * V * J * I + 2 * U * V * I

F32 = mybir.dt.float32
BF16 = mybir.dt.bfloat16
I32 = mybir.dt.int32
U32 = mybir.dt.uint32
U8 = mybir.dt.uint8
FP8X4 = mybir.dt.float8_e4m3fn_x4
FP4X4 = mybir.dt.float4_e2m1fn_x4
ACT = mybir.ActivationFunctionType
ALU = mybir.AluOpType

P = 128
SLOTS = 4
GROUP = P * SLOTS
JG, VG, UG, IG = J // GROUP, V // GROUP, U // GROUP, I // GROUP
QUADRANTS, QUADRANT, SCALE_ROWS = 4, 32, 4
BANKS = 8
RUN = 4


def tile_user_neighbour_rating_prediction_k4_kernel(
    tc, x_words, x_scales, prof, e_words, e_scales, h, dev, conf, gain, off, out_0, out_1, out_2
):
    nc = tc.nc
    with ExitStack() as ctx:
        keep = ctx.enter_context(tc.tile_pool(name="keep", bufs=1))
        work = ctx.enter_context(tc.tile_pool(name="work", bufs=3))
        psum = ctx.enter_context(tc.psum_pool(name="psum", bufs=1))
        ctx.enter_context(tc.manual_schedule())

        def kept(name, shape, dtype):
            return keep.tile(shape, dtype, name=name, align_bytes=64)

        def group(g):
            return slice(g * GROUP, (g + 1) * GROUP)

        def block(b):
            return slice(b * P, (b + 1) * P)

        ident = kept("ident", [P, P], F32)
        e_plane = kept("e_plane", [P, JG, I], U8)
        x_plane = kept("x_plane", [P, U], U8)
        nc.vector.memset(e_plane[:].rearrange("p g n -> p (g n)").bitcast(I32), 0)
        nc.vector.memset(x_plane[:].bitcast(I32), 0)
        make_identity(nc, ident[:])

        dev_sb = kept("dev_sb", [P, VG, SLOTS], BF16)
        gain_raw = kept("gain_raw", [P, IG, SLOTS], BF16)
        off_raw = kept("off_raw", [P, IG, SLOTS], BF16)
        gain_sb = kept("gain_sb", [P, IG, SLOTS], F32)
        off_sb = kept("off_sb", [P, IG, SLOTS], F32)
        conf_row = kept("conf_row", [P, U], BF16)
        prof_sb, x_sb, e_sb, h_sb = {}, {}, {}, {}

        def load_prof(vg, slots):
            rows = prof[group(vg), :].rearrange("(m t) k -> m t k", t=SLOTS)
            for t in slots:
                prof_sb[vg, t] = kept("prof_%d_%d" % (vg, t), [P, J], BF16)
                nc.sync.dma_start(out=prof_sb[vg, t][:], in_=rows[:, t, :])

        def load_x(ug):
            x_sb[ug] = kept("x_%d" % ug, [P, JG, GROUP], U32)
            words = x_words.rearrange("g p n t -> p g (n t)").bitcast(I32)
            nc.sync.dma_start(out=x_sb[ug][:].bitcast(I32), in_=words[:, :, group(ug)])

        def load_e(ig):
            e_sb[ig] = kept("e_%d" % ig, [P, JG, 2 * GROUP], U8)
            src = e_words.rearrange("g p b -> p g b")[:, :, 2 * ig * GROUP : 2 * (ig + 1) * GROUP]
            nc.sync.dma_start(out=e_sb[ig][:].bitcast(I32), in_=src.bitcast(I32))

        def load_h(vg, ug):
            h_sb[vg, ug] = kept("h_%d_%d" % (vg, ug), [P, SLOTS, GROUP], BF16)
            nc.sync.dma_start(out=h_sb[vg, ug][:], in_=h[group(vg), group(ug)].rearrange("(p t) u -> p t u", t=SLOTS))

        def scale_rows(q):
            return slice(SCALE_ROWS * q, SCALE_ROWS * (q + 1))

        def live_rows(q, planes):
            return slice(QUADRANT * q, QUADRANT * q + SCALE_ROWS * planes)

        load_prof(0, (0, 1))
        for q in range(QUADRANTS):
            nc.sync.dma_start(
                out=e_plane[live_rows(q, 1), :, :].bitcast(I32),
                in_=e_scales[:, scale_rows(q), :].rearrange("g r n -> r g n").bitcast(I32),
            )
        load_prof(0, (2, 3))
        nc.sync.dma_start(out=dev_sb[:], in_=dev.rearrange("(g p t) -> p g t", p=P, t=SLOTS))
        load_e(0)
        load_h(0, 0)
        load_x(0)
        for q in range(QUADRANTS):
            nc.sync.dma_start(out=x_plane[live_rows(q, JG), :].bitcast(I32), in_=x_scales[:, scale_rows(q), :].bitcast(I32))
        load_prof(1, range(SLOTS))
        load_h(1, 0)
        load_e(1)
        load_x(1)
        load_h(0, 1)
        load_h(1, 1)
        load_e(2)
        nc.sync.dma_start(out=gain_raw[:], in_=gain.rearrange("(g p t) -> p g t", p=P, t=SLOTS))
        nc.sync.dma_start(out=off_raw[:], in_=off.rearrange("(g p t) -> p g t", p=P, t=SLOTS))
        nc.sync.dma_start(out=conf_row[:], in_=conf.partition_broadcast(P))

        later = {}
        clock = [0]

        def after(steps, *call):
            later.setdefault(clock[0] + steps, []).append(call)

        def step(job, *followers):
            for call in later.get(clock[0], []):
                call[0](*call[1:])
            job[0](*job[1:])
            for call in followers:
                after(1, *call)
            clock[0] = clock[0] + 1

        def pause():
            return None

        def next_bank():
            return psum.tile([P, SLOTS, P], F32, name="bank", tag="bank%d" % (clock[0] % BANKS))

        def quantize(codes, plane, src):
            nc.vector.quantize_mx(out=codes.bitcast(FP8X4), scales=plane, in_=src)

        def interleave(dst, src):
            nc.scalar.copy(
                out=dst.rearrange("p (c i) t -> p c t i", i=RUN), in_=src.rearrange("p t (c i) -> p c t i", i=RUN)
            )

        b_bf = [kept("b_bf_%d" % vg, [P, SLOTS, JG * GROUP], BF16) for vg in range(VG)]
        b_codes = [kept("b_codes_%d" % vg, [P, SLOTS, JG, P], U32) for vg in range(VG)]
        b_plane = [kept("b_plane_%d" % vg, [P, SLOTS, JG, P], U8) for vg in range(VG)]

        def turn_prof(vg, t):
            bank = next_bank()
            words = prof_sb[vg, t][:].bitcast(F32)
            for jg in range(JG):
                for e in range(2):
                    nc.tensor.transpose(bank[:, 2 * jg + e, :], words[:, 2 * P * jg + e : 2 * P * (jg + 1) : 2], ident[:])
            after(1, pair_words, bank, vg, t)

        def pair_words(bank, vg, t):
            nc.scalar.copy(
                out=b_bf[vg][:, t, :].bitcast(F32).rearrange("p (g m e) -> p g m e", g=JG, e=2),
                in_=bank[:].rearrange("p (g e) m -> p g m e", e=2),
            )

        def quantize_b(vg, first, last):
            quantize(
                b_codes[vg][:, first : last + 1].rearrange("p t g m -> p (t g m)"),
                b_plane[vg][:, first : last + 1].rearrange("p t g m -> p (t g m)"),
                b_bf[vg][:, first : last + 1].rearrange("p t k -> p (t k)"),
            )

        def first_stage(vg, moving, planes):
            bank = next_bank()
            for t in range(SLOTS):
                for jg in range(JG):
                    nc.tensor.matmul_mx(
                        out=bank[:, t, :],
                        lhsT=b_codes[vg][:, t, jg, :].bitcast(FP8X4),
                        lhsT_scale=b_plane[vg][:, t, jg, :],
                        rhs=moving[jg],
                        rhs_scale=planes[jg],
                        start=(jg == 0),
                        stop=(jg == JG - 1),
                    )
            return bank

        h_words, w_factors, w_bf, w_codes, w_plane = {}, {}, {}, {}, {}

        def order_h(vg, ug, pair):
            if pair == 0:
                h_words[vg, ug] = work.tile([P, GROUP, SLOTS], BF16, name="h_words")
            users = slice(2 * P * pair, 2 * P * (pair + 1))
            interleave(h_words[vg, ug][:, users, :], h_sb[vg, ug][:, :, users])

        def w_block(vg, ug, b):
            u0 = ug * GROUP + b * P
            bank = first_stage(
                vg,
                [x_sb[ug][:, jg, block(b)].bitcast(FP8X4) for jg in range(JG)],
                [x_plane[SCALE_ROWS * jg : P, u0 : u0 + P] for jg in range(JG)],
            )
            if b % 2 == 0:
                cos_h = work.tile([P, 2 * P, SLOTS], F32, name="cos_h")
                cos_abs = work.tile([P, 2 * P, SLOTS], F32, name="cos_abs")
                w_factors[vg, ug, b // 2] = (cos_h, cos_abs)
            after(1, shrink, bank, vg, ug, b)
            after(2, magnitude, bank, vg, ug, b)

        def shrink(bank, vg, ug, b):
            nc.vector.tensor_tensor(
                out=w_factors[vg, ug, b // 2][0][:, block(b % 2), :],
                in0=bank[:].rearrange("p t u -> p u t"),
                in1=h_words[vg, ug][:, block(b), :],
                op=ALU.mult,
            )

        def magnitude(bank, vg, ug, b):
            nc.scalar.activation(
                out=w_factors[vg, ug, b // 2][1][:, block(b % 2), :], in_=bank[:].rearrange("p t u -> p u t"), func=ACT.Abs
            )

        def finish_w(vg, ug, pair):
            if pair == 0:
                w_bf[vg, ug] = work.tile([P, GROUP, SLOTS], BF16, name="w_bf", align_bytes=64, bufs=1)
            cos_h, cos_abs = w_factors[vg, ug, pair]
            users = slice(2 * P * pair, 2 * P * (pair + 1))
            nc.gpsimd.tensor_tensor(out=w_bf[vg, ug][:, users, :], in0=cos_h[:], in1=cos_abs[:], op=ALU.mult)

        def quantize_w(vg, ug):
            w_codes[vg, ug] = kept("w_codes_%d_%d" % (vg, ug), [P, GROUP], U32)
            w_plane[vg, ug] = kept("w_plane_%d_%d" % (vg, ug), [P, GROUP], U8)
            quantize(w_codes[vg, ug][:], w_plane[vg, ug][:], w_bf[vg, ug][:].rearrange("p u t -> p (u t)"))

        c_bf, c_codes, c_plane = {}, {}, {}
        per_block = P // SLOTS

        def c_block(vg, ig, b):
            i0 = ig * GROUP + b * P
            bank = first_stage(
                vg,
                [e_sb[ig][:, jg, 2 * b * P : 2 * (b + 1) * P].bitcast(FP4X4) for jg in range(JG)],
                [e_plane[:, jg, i0 : i0 + P] for jg in range(JG)],
            )
            if b == 0:
                c_bf[vg, ig] = work.tile([P, SLOTS, P, SLOTS], BF16, name="c_bf", align_bytes=64)
            after(1, scale_c, bank, vg, ig, b)

        def scale_c(bank, vg, ig, b):
            dev_slots = dev_sb[:, vg, :].rearrange("p (m s t) -> p m s t", m=1, s=1)
            nc.vector.tensor_tensor(
                out=c_bf[vg, ig][:, :, per_block * b : per_block * (b + 1), :].rearrange("p s m t -> p m s t"),
                in0=bank[:].rearrange("p t (m s) -> p m s t", s=SLOTS),
                in1=dev_slots.to_broadcast([P, per_block, SLOTS, SLOTS]),
                op=ALU.mult,
            )

        def quantize_c(vg, ig):
            c_codes[vg, ig] = kept("c_codes_%d_%d" % (vg, ig), [P, GROUP], U32)
            c_plane[vg, ig] = kept("c_plane_%d_%d" % (vg, ig), [P, GROUP], U8)
            quantize(c_codes[vg, ig][:], c_plane[vg, ig][:], c_bf[vg, ig][:].rearrange("p s m t -> p (s m t)"))

        y_t, y_bf, y_codes = {}, {}, {}
        y_planes = [kept("y_plane_a", [P, U], U8), kept("y_plane_b", [P, U], U8)]

        def widen_gain_off():
            nc.scalar.copy(out=gain_sb[:], in_=gain_raw[:])
            nc.scalar.copy(out=off_sb[:], in_=off_raw[:])

        def predict(unit, s, by_item):
            ig, ug = unit
            bank = next_bank()[:].rearrange("p a b -> p (a b)")
            for vg in range(VG):
                nc.tensor.matmul_mx(
                    out=bank,
                    lhsT=c_codes[vg, ig][:, block(s)].bitcast(FP8X4),
                    lhsT_scale=c_plane[vg, ig][:, block(s)],
                    rhs=w_codes[vg, ug][:].bitcast(FP8X4),
                    rhs_scale=w_plane[vg, ug][:],
                    start=(vg == 0),
                    stop=(vg == VG - 1),
                )
            p_conf = work.tile([P, GROUP], F32, name="p_conf", bufs=4)
            if s == 0:
                y_t[unit] = work.tile([P, SLOTS, GROUP], F32, name="y_t")
            after(1, by_user, bank, p_conf, ug)
            after(2, by_item, p_conf, unit, s)

        def by_user(bank, p_conf, ug):
            nc.vector.tensor_tensor(out=p_conf[:], in0=bank, in1=conf_row[:, group(ug)], op=ALU.mult)

        def by_item_on_scalar(p_conf, unit, s):
            nc.scalar.activation(
                out=y_t[unit][:, s, :],
                in_=p_conf[:],
                func=ACT.Identity,
                scale=gain_sb[:, unit[0], s : s + 1],
                bias=off_sb[:, unit[0], s : s + 1],
            )

        def by_item_on_gpsimd(p_conf, unit, s):
            nc.gpsimd.tensor_scalar(
                out=y_t[unit][:, s, :],
                in0=p_conf[:],
                scalar1=gain_sb[:, unit[0], s : s + 1],
                scalar2=off_sb[:, unit[0], s : s + 1],
                op0=ALU.mult,
                op1=ALU.add,
            )

        def turn_y(unit, b, copy):
            bank = next_bank()
            for s in range(SLOTS):
                nc.tensor.transpose(bank[:, s, :], y_t[unit][:, s, block(b)], ident[:])
            y_rows = work.tile([P, GROUP], F32, name="y_rows", bufs=6)
            after(1, store_y, bank, y_rows, unit, b, copy)

        def store_y(bank, y_rows, unit, b, copy):
            ig, ug = unit
            copy(out=y_rows[:].rearrange("p (m s) -> p m s", s=SLOTS), in_=bank[:].rearrange("p s m -> p m s"))
            u0 = ug * GROUP + b * P
            nc.sync.dma_start(out=out_0[u0 : u0 + P, group(ig)], in_=y_rows[:])

        def round_y(unit, b):
            if unit not in y_bf:
                y_bf[unit] = work.tile([P, GROUP, SLOTS], BF16, name="y_bf", align_bytes=64)
            interleave(y_bf[unit][:, block(b), :], y_t[unit][:, :, block(b)])

        def quantize_y(unit):
            ig, ug = unit
            y_codes[unit] = work.tile([P, GROUP], U32, name="y_codes", align_bytes=64)
            plane = y_planes[ig // 2][SCALE_ROWS * (ig % 2) : P, group(ug)]
            quantize(y_codes[unit][:], plane, y_bf[unit][:].rearrange("p u t -> p (u t)"))

        def store_codes(unit):
            ig, ug = unit
            words = out_1[ig].rearrange("p m t -> p (m t)").bitcast(I32)
            nc.sync.dma_start(out=words[:, group(ug)], in_=y_codes[unit][:].bitcast(I32))

        def store_planes(first, count):
            for q in range(QUADRANTS):
                nc.sync.dma_start(
                    out=out_2[first : first + count, scale_rows(q), :].bitcast(I32),
                    in_=y_planes[first // 2][live_rows(q, count), :].bitcast(I32),
                )

        on_scalar, on_vector = nc.scalar.copy, nc.vector.tensor_copy

        def weave(first, second, followers):
            jobs = [job for both in zip(first, second) for job in both]
            for n, job in enumerate(jobs):
                step(job, *followers.get(n, []))

        def w_blocks(vg, ug):
            return [(w_block, vg, ug, b) for b in range(SLOTS)]

        def c_blocks(vg, ig):
            return [(c_block, vg, ig, b) for b in range(SLOTS)]

        step((turn_prof, 0, 0))
        for t in range(1, SLOTS):
            step((turn_prof, 0, t), (quantize_b, 0, t - 1, t - 1))
        step((pause,), (quantize_b, 0, SLOTS - 1, SLOTS - 1), (order_h, 0, 0, 0), (order_h, 0, 0, 1))
        step((pause,))

        weave(c_blocks(0, 0)[:3], w_blocks(0, 0)[:3], {})
        step((turn_prof, 1, 0), (finish_w, 0, 0, 0))
        step((turn_prof, 1, 1))
        step((c_block, 0, 0, 3))
        step((turn_prof, 1, 2))
        step((turn_prof, 1, 3), (quantize_c, 0, 0))
        step((w_block, 0, 0, 3), (quantize_b, 1, 0, SLOTS - 1), (order_h, 1, 0, 0))
        step((c_block, 0, 1, 0), (order_h, 1, 0, 1))
        step((c_block, 0, 1, 1), (finish_w, 0, 0, 1))
        step((c_block, 0, 1, 2))
        step((c_block, 0, 1, 3))

        weave(
            w_blocks(1, 0),
            c_blocks(1, 0),
            {
                1: [(order_h, 0, 1, 0)],
                4: [(quantize_w, 0, 0), (quantize_c, 0, 1), (finish_w, 1, 0, 0)],
                5: [(order_h, 0, 1, 1)],
                7: [(widen_gain_off,)],
            },
        )
        weave(
            w_blocks(0, 1),
            c_blocks(1, 1),
            {
                0: [(finish_w, 1, 0, 1)],
                1: [(order_h, 1, 1, 0)],
                4: [(quantize_w, 1, 0), (quantize_c, 1, 0), (finish_w, 0, 1, 0)],
                5: [(order_h, 1, 1, 1)],
            },
        )
        weave(
            w_blocks(1, 1),
            [(predict, (0, 0), s, by_item_on_scalar) for s in range(SLOTS)],
            {0: [(finish_w, 0, 1, 1)], 4: [(quantize_c, 1, 1), (quantize_w, 0, 1), (finish_w, 1, 1, 0)]},
        )

        step((predict, (1, 0), 0, by_item_on_scalar), (finish_w, 1, 1, 1), (round_y, (0, 0), 0))
        step((predict, (1, 0), 1, by_item_on_scalar), (round_y, (0, 0), 1))
        step((c_block, 0, 2, 0))
        step((c_block, 0, 2, 1))
        step((turn_y, (0, 0), 0, on_scalar))
        step((turn_y, (0, 0), 1, on_scalar))
        step((predict, (1, 0), 2, by_item_on_scalar), (round_y, (0, 0), 2))
        step((predict, (1, 0), 3, by_item_on_gpsimd), (quantize_w, 1, 1), (round_y, (0, 0), 3))
        step((c_block, 0, 2, 2))
        step((c_block, 0, 2, 3))
        step((turn_y, (0, 0), 2, on_scalar))
        step((turn_y, (0, 0), 3, on_scalar))
        step((c_block, 1, 2, 0), (quantize_c, 0, 2))
        step((c_block, 1, 2, 1))

        units = [(0, 0), (1, 0), (0, 1), (1, 1), (2, 0), (2, 1)]
        for n in range(2, len(units)):
            unit, before, oldest = units[n], units[n - 1], units[n - 2]
            with_c, last = n == 2, n == len(units) - 1
            stores = [(store_codes, oldest)] + ([(store_planes, 0, 2)] if oldest == (1, 1) else [])
            step((predict, unit, 0, by_item_on_gpsimd), (quantize_y, oldest), (round_y, before, 0))
            step((predict, unit, 1, by_item_on_gpsimd), *stores, (round_y, before, 1))
            step((turn_y, before, 0, on_scalar))
            step((turn_y, before, 1, on_scalar))
            step((predict, unit, 2, by_item_on_gpsimd), (round_y, before, 2))
            step((predict, unit, 3, by_item_on_scalar), (round_y, before, 3))
            if with_c:
                step((c_block, 1, 2, 2))
                step((c_block, 1, 2, 3))
                step((turn_y, before, 2, on_scalar))
                step((turn_y, before, 3, on_scalar), (quantize_c, 1, 2))
            else:
                step((turn_y, before, 2, on_vector))
                step((turn_y, before, 3, on_vector), *([(round_y, unit, 0)] if last else []))

        unit, before = units[-1], units[-2]
        step((turn_y, unit, 0, on_scalar), (quantize_y, before), (round_y, unit, 1))
        step((turn_y, unit, 1, on_vector), (store_codes, before), (round_y, unit, 2))
        step((turn_y, unit, 2, on_vector), (round_y, unit, 3))
        step((turn_y, unit, 3, on_vector), (quantize_y, unit), (store_codes, unit), (store_planes, 2, 1))
        step((pause,))
